import numpy as np
import ml_dtypes


def mxq(x, axis, fmt="e4m3"):
    dtype, down = {"e4m3": (ml_dtypes.float8_e4m3fn, 7), "e5m2": (ml_dtypes.float8_e5m2, 14)}[fmt]
    v = np.moveaxis(np.asarray(x, np.float32).astype(ml_dtypes.bfloat16).astype(np.float64), axis, -1)
    blocks = v.reshape(v.shape[:-1] + (-1, 32))
    amax = np.abs(blocks).max(-1, keepdims=True)
    byte = np.maximum(np.where(amax > 0, np.frexp(amax)[1] - 1 + 127, 0) - down, 1)
    scale = np.exp2(byte - 127.0)
    codes = (blocks / scale).astype(np.float32).astype(dtype).astype(np.float64)
    return np.moveaxis((codes * scale).reshape(v.shape), -1, axis)


WIDE = False


def mx_kscale(k):
    if not WIDE:
        return np.ones(k)
    levels = np.array([10, -10, 5, -5, 0])
    if k % 512:
        return np.exp2(np.random.permutation(np.resize(levels, k // 32))).repeat(32)
    a = np.empty((k // 512, 16))
    for p in range(k // 512):
        a[p, :8] = np.random.permutation(np.resize(levels, 8))
        for g in range(8):
            far = levels[np.abs(levels - a[p, g]) >= 10]
            a[p, g + 8] = far[np.random.randint(len(far))]
    return np.exp2(a.ravel()).repeat(32)


def f64(x):
    return np.asarray(x).astype(np.float64)


def striped(idx):
    return np.tile(idx.reshape(-1, 16).T, (8, 1)).astype(np.uint16)


def unstriped(offs):
    return offs[:16].T.reshape(-1).astype(np.int64)


def pack_weight(w):
    k, n = w.shape
    w = f64(np.asarray(w, np.float32).astype(ml_dtypes.bfloat16)).reshape(k // 32, 32, n)
    amax = np.abs(w).max(1)
    byte = np.clip(np.where(amax > 0, np.frexp(amax)[1] - 1 + 127 - 7, 1), 1, 254)
    scaled = (w * np.exp2(127.0 - byte)[:, None, :]).reshape(k, n).astype(np.float32)
    words = np.ascontiguousarray(scaled.reshape(k // 512, 128, 4, n).transpose(0, 1, 3, 2)).astype(ml_dtypes.float8_e4m3fn).view(np.uint8)
    return words, np.ascontiguousarray(byte.astype(np.uint8).reshape(k // 512, 16, n))


def unpack_weight(words, scales):
    g, p, n, _ = words.shape
    vals = np.ascontiguousarray(words).view(ml_dtypes.float8_e4m3fn).astype(np.float64) * np.repeat(np.exp2(scales.astype(np.float64) - 127.0), 8, axis=1)[..., None]
    return vals.transpose(0, 1, 3, 2).reshape(g * 512, n)


def sigmoid(v):
    return 1.0 / (1.0 + np.exp(-np.maximum(v, -700.0)))

def planes(y):
    n, m = y.shape
    v = y.astype(np.float32).astype(ml_dtypes.bfloat16).astype(np.float64).reshape(n // 32, 32, m)
    top = np.abs(v).max(1)
    byte = np.clip(np.where(top > 0, np.frexp(top)[1] - 1 + 127 - 7, 1), 1, 254)
    codes = (v * np.exp2(127.0 - byte)[:, None, :]).reshape(n, m).astype(np.float32).astype(ml_dtypes.float8_e4m3fn).view(np.uint8)
    words = codes.reshape(n // 512, 128, 4, m).transpose(0, 1, 3, 2)
    return np.ascontiguousarray(words), np.ascontiguousarray(byte.astype(np.uint8).reshape(n // 512, 16, m))


K, T, S, N, U = 512, 2048, 1024, 512, 1024


def setup_inputs():
    n = np.random.standard_normal
    s = mx_kscale(K)[:, None]
    packed_xT = pack_weight(n((K, T)) * s)
    return {
        "x_words": packed_xT[0],
        "x_scales": packed_xT[1],
        "w1": (n((K, N)) / np.sqrt(K) / s).astype(np.float32),
        "w2": (n((K, N)) / np.sqrt(K) / s).astype(np.float32),
        "w3": (n((K, N)) / np.sqrt(K) / s).astype(np.float32),
        "offs": striped(np.random.permutation(T)[:S]),
        "src": striped(np.random.permutation(S)[(S * np.random.uniform(0, 1, U) ** 4).astype(np.int64)]),
        "dst": striped(np.random.permutation(S)),
    }


def reference(x_words, x_scales, w1, w2, w3, offs, src, dst):
    xq = unpack_weight(x_words, x_scales)[:, unstriped(offs)]
    y = mxq(f64(w1), 0, "e4m3").T @ xq
    e = mxq(f64(w2), 0, "e4m3").T @ xq
    h = mxq(f64(w3), 0, "e4m3").T @ xq
    out_0 = (sigmoid(y[:, unstriped(dst)] + e[:, unstriped(src)])) * h[:, unstriped(src)]
    return (out_0,) + planes(out_0)

@@ -1,0 +1,201 @@
+from contextlib import ExitStack
+
+import concourse.mybir as mybir
+
+K, T, S, N, U = 512, 2048, 1024, 512, 1024
+FLOPS = 3 * 2 * K * N * S
+
+F32 = mybir.dt.float32
+BF16 = mybir.dt.bfloat16
+I32 = mybir.dt.int32
+U32 = mybir.dt.uint32
+U16 = mybir.dt.uint16
+U8 = mybir.dt.uint8
+FP8X4 = mybir.dt.float8_e4m3fn_x4
+ADD = mybir.AluOpType.add
+MULT = mybir.AluOpType.mult
+SIGMOID = mybir.ActivationFunctionType.Sigmoid
+
+P = 128
+PACK = 4
+BANK = 512
+LIST_ROWS = 16
+EDGE_CHUNKS = (256, 256, 256, 128, 128)
+
+
+def tile_picked_edgeatt_sigmoid_po_kernel(
+    tc, x_words, x_scales, w1, w2, w3, offs, src, dst, out_0, out_1, out_2
+):
+    nc = tc.nc
+    with ExitStack() as ctx:
+        keep = ctx.enter_context(tc.tile_pool(name="keep", bufs=1))
+        psum = ctx.enter_context(tc.psum_pool(name="psum", bufs=8))
+
+        def entries(lst, first, count):
+            return lst[:, first // LIST_ROWS : (first + count) // LIST_ROWS]
+
+        offs_sb = keep.tile([P, S // LIST_ROWS], U16, name="offs_sb")
+        src_sb = keep.tile([P, U // LIST_ROWS], U16, name="src_sb")
+        dst_sb = keep.tile([P, U // LIST_ROWS], U16, name="dst_sb")
+        words_all = keep.tile([P, T], U32, name="words_all", align_bytes=64)
+        scales_all = keep.tile([P, T], U8, name="scales_all", align_bytes=64)
+
+        nc.vector.memset(scales_all[:].bitcast(I32), 0)
+        nc.sync.dma_start(offs_sb[:], offs)
+        for q in range(4):
+            nc.scalar.dma_start(
+                scales_all[32 * q : 32 * q + 4, :].bitcast(I32), x_scales[0, 4 * q : 4 * q + 4, :].bitcast(I32)
+            )
+        nc.sync.dma_start(words_all[:].bitcast(I32), x_words[0].rearrange("p c r -> p (c r)").bitcast(I32))
+
+        def load_weight(w, name, pieces):
+            width = N // pieces
+            tiles = []
+            for i in range(pieces):
+                raw = keep.tile([P, PACK, width], F32, name=f"{name}_raw{i}")
+                nc.sync.dma_start(raw[:], w.rearrange("(p j) c -> p j c", j=PACK)[:, :, i * width : (i + 1) * width])
+                tiles.append(raw)
+            return tiles
+
+        w1_raw = load_weight(w1, "w1", 2)
+        nc.sync.dma_start(dst_sb[:], dst)
+        nc.sync.dma_start(src_sb[:], src)
+        w2_raw = load_weight(w2, "w2", 1)
+        w3_raw = load_weight(w3, "w3", 1)
+
+        table = keep.tile([P, 1], F32, name="table")
+        nc.gpsimd.memset(table[:], 0.0)
+        table_out = keep.tile([P, 1], F32, name="table_out")
+        nc.scalar.activation(table_out[:], table[:], SIGMOID)
+
+        def deal_weight(raws, name):
+            dealt = keep.tile([P, PACK, P, PACK], BF16, name=f"{name}_dealt", align_bytes=64)
+            step = P // len(raws)
+            for i, raw in enumerate(raws):
+                nc.scalar.copy(
+                    dealt[:, :, i * step : (i + 1) * step, :].rearrange("p t m j -> p m t j"),
+                    raw[:].rearrange("p j (m t) -> p m t j", t=PACK),
+                )
+            return dealt
+
+        def quantise_weight(dealt, name, cuts):
+            codes = keep.tile([P, N], U32, name=f"{name}_codes", align_bytes=64)
+            scales = keep.tile([P, N], U8, name=f"{name}_scales", align_bytes=64)
+            for t0, t1 in cuts:
+                nc.vector.quantize_mx(
+                    out=codes[:, t0 * P : t1 * P].bitcast(FP8X4),
+                    scales=scales[:, t0 * P : t1 * P],
+                    in_=dealt[:, t0:t1, :, :].rearrange("p t m j -> p (t m j)"),
+                )
+            return codes, scales
+
+        x_codes = keep.tile([P, S], U32, name="x_codes", align_bytes=64)
+        x_bytes = keep.tile([P, S], U8, name="x_bytes", align_bytes=64)
+        nc.vector.tensor_copy(x_bytes[:], scales_all[:].indirect(offs_sb[:]))
+        for c0 in range(0, S, BANK):
+            nc.vector.tensor_copy(x_codes[:, c0 : c0 + BANK], words_all[:].indirect(entries(offs_sb, c0, BANK)))
+
+        def product(weight, t, name, first=False):
+            codes, scales = weight
+            rows = keep.tile([P, S], F32, name=f"{name}{t}")
+            for c0 in range(0, S, BANK):
+                acc = psum.tile([P, BANK], F32, name="acc")
+                nc.tensor.matmul_mx(
+                    out=acc[:],
+                    lhsT=codes[:, t * P : (t + 1) * P].bitcast(FP8X4),
+                    lhsT_scale=scales[:, t * P : (t + 1) * P],
+                    rhs=x_codes[:, c0 : c0 + BANK].bitcast(FP8X4),
+                    rhs_scale=x_bytes[:, c0 : c0 + BANK],
+                    start=True,
+                    stop=True,
+                )
+                if first and c0 > 0:
+                    nc.vector.tensor_copy(rows[:, c0 : c0 + BANK], acc[:])
+                else:
+                    nc.scalar.copy(rows[:, c0 : c0 + BANK], acc[:])
+            return rows
+
+        y_dst = [keep.tile([P, U], F32, name=f"y_dst{t}") for t in range(PACK)]
+        logit = [keep.tile([P, U], F32, name=f"logit{t}") for t in range(PACK)]
+        gate = [keep.tile([P, U], F32, name=f"gate{t}") for t in range(PACK)]
+
+        def fetch_y(y, t):
+            for c0 in range(0, U, BANK):
+                nc.vector.tensor_copy(y_dst[t][:, c0 : c0 + BANK], y[:].indirect(entries(dst_sb, c0, BANK)))
+
+        def add_e(e, t):
+            for c0 in range(0, U, BANK):
+                nc.vector.tensor_tensor(
+                    logit[t][:, c0 : c0 + BANK], e[:].indirect(entries(src_sb, c0, BANK)), y_dst[t][:, c0 : c0 + BANK], ADD
+                )
+
+        def squash(t, c0):
+            nc.scalar.activation(gate[t][:, c0 : c0 + BANK], logit[t][:, c0 : c0 + BANK], SIGMOID)
+
+        w1_mx = quantise_weight(deal_weight(w1_raw, "w1"), "w1", [(0, 1), (1, 2), (2, 4)])
+        y0 = product(w1_mx, 0, "y", first=True)
+        y1 = product(w1_mx, 1, "y")
+        fetch_y(y0, 0)
+        y2 = product(w1_mx, 2, "y")
+        fetch_y(y1, 1)
+        w2_dealt = deal_weight(w2_raw, "w2")
+        y3 = product(w1_mx, 3, "y")
+        fetch_y(y2, 2)
+        w2_mx = quantise_weight(w2_dealt, "w2", [(0, 4)])
+        e0 = product(w2_mx, 0, "e")
+        fetch_y(y3, 3)
+        e1 = product(w2_mx, 1, "e")
+        add_e(e0, 0)
+        w3_dealt = deal_weight(w3_raw, "w3")
+        e2 = product(w2_mx, 2, "e")
+        add_e(e1, 1)
+        w3_mx = quantise_weight(w3_dealt, "w3", [(0, 4)])
+        e3 = product(w2_mx, 3, "e")
+        add_e(e2, 2)
+        h = [product(w3_mx, t, "h") for t in range(PACK)]
+        add_e(e3, 3)
+        for c0 in range(0, U, BANK):
+            for t in range(PACK):
+                squash(t, c0)
+
+        out_codes = keep.tile([P, U], U32, name="out_codes", align_bytes=64)
+        out_scales = keep.tile([P, U], U8, name="out_scales", align_bytes=64)
+        out_rows = out_0.rearrange("(p t) c -> p t c", t=PACK)
+        out_words = out_1[0].rearrange("p c r -> p (c r)").bitcast(I32)
+
+        def messages(c0, n):
+            msg = keep.tile([P, PACK, n], F32, name=f"msg{c0}")
+            for t in range(PACK):
+                nc.vector.tensor_tensor(
+                    msg[:, t, :], h[t][:].indirect(entries(src_sb, c0, n)), gate[t][:, c0 : c0 + n], MULT
+                )
+            nc.sync.dma_start(out_rows[:, :, c0 : c0 + n], msg[:])
+            rounded = keep.tile([P, n, PACK], BF16, name=f"rounded{c0}", align_bytes=64)
+            copy = nc.vector.tensor_copy if c0 + n == U else nc.scalar.copy
+            copy(
+                rounded[:].rearrange("p (c i) t -> p c t i", i=4),
+                msg[:].rearrange("p t (c i) -> p c t i", i=4),
+            )
+            return rounded
+
+        def planes(rounded, c0, n):
+            nc.vector.quantize_mx(
+                out=out_codes[:, c0 : c0 + n].bitcast(FP8X4),
+                scales=out_scales[:, c0 : c0 + n],
+                in_=rounded[:].rearrange("p c t -> p (c t)"),
+            )
+            nc.sync.dma_start(out_words[:, c0 : c0 + n], out_codes[:, c0 : c0 + n].bitcast(I32))
+
+        waiting = None
+        c0 = 0
+        for n in EDGE_CHUNKS:
+            rounded = messages(c0, n)
+            if waiting is not None:
+                planes(*waiting)
+            waiting = (rounded, c0, n)
+            c0 = c0 + n
+        planes(*waiting)
+        for q in range(4):
+            nc.scalar.dma_start(
+                out_2[0, 4 * q : 4 * q + 4, :].bitcast(I32), out_scales[32 * q : 32 * q + 4, :].bitcast(I32)
+            )

@@ -20,7 +20,7 @@ P = 128
 PACK = 4
 BANK = 512
 LIST_ROWS = 16
-EDGE_CHUNKS = (256, 256, 256, 128, 128)
+SPARE = {"y": 352, "e": 16, "h": 0}
 
 
 def tile_picked_edgeatt_sigmoid_po_kernel(
@@ -41,27 +41,25 @@ def tile_picked_edgeatt_sigmoid_po_kernel(
         scales_all = keep.tile([P, T], U8, name="scales_all", align_bytes=64)
 
         nc.vector.memset(scales_all[:].bitcast(I32), 0)
+
+        def load_weight(w, name, c0, c1):
+            raw = keep.tile([P, PACK, c1 - c0], F32, name=f"{name}_raw{c0}")
+            nc.sync.dma_start(raw[:], w.rearrange("(p j) c -> p j c", j=PACK)[:, :, c0:c1])
+            return raw, c0, c1
+
         nc.sync.dma_start(offs_sb[:], offs)
+        w1_raw = [load_weight(w1, "w1", 0, 128)]
         for q in range(4):
-            nc.scalar.dma_start(
+            nc.sync.dma_start(
                 scales_all[32 * q : 32 * q + 4, :].bitcast(I32), x_scales[0, 4 * q : 4 * q + 4, :].bitcast(I32)
             )
         nc.sync.dma_start(words_all[:].bitcast(I32), x_words[0].rearrange("p c r -> p (c r)").bitcast(I32))
-
-        def load_weight(w, name, pieces):
-            width = N // pieces
-            tiles = []
-            for i in range(pieces):
-                raw = keep.tile([P, PACK, width], F32, name=f"{name}_raw{i}")
-                nc.sync.dma_start(raw[:], w.rearrange("(p j) c -> p j c", j=PACK)[:, :, i * width : (i + 1) * width])
-                tiles.append(raw)
-            return tiles
-
-        w1_raw = load_weight(w1, "w1", 2)
+        w1_raw.append(load_weight(w1, "w1", 128, 320))
+        w1_raw.append(load_weight(w1, "w1", 320, 512))
         nc.sync.dma_start(dst_sb[:], dst)
+        w2_raw = [load_weight(w2, "w2", 0, N)]
         nc.sync.dma_start(src_sb[:], src)
-        w2_raw = load_weight(w2, "w2", 1)
-        w3_raw = load_weight(w3, "w3", 1)
+        w3_raw = [load_weight(w3, "w3", 0, N)]
 
         table = keep.tile([P, 1], F32, name="table")
         nc.gpsimd.memset(table[:], 0.0)
@@ -70,11 +68,15 @@ def tile_picked_edgeatt_sigmoid_po_kernel(
 
         def deal_weight(raws, name):
             dealt = keep.tile([P, PACK, P, PACK], BF16, name=f"{name}_dealt", align_bytes=64)
-            step = P // len(raws)
-            for i, raw in enumerate(raws):
-                nc.scalar.copy(
-                    dealt[:, :, i * step : (i + 1) * step, :].rearrange("p t m j -> p m t j"),
-                    raw[:].rearrange("p j (m t) -> p m t j", t=PACK),
+            if len(raws) == 1:
+                parts = [(raws[0], 0, PACK, nc.scalar.copy)]
+            else:
+                parts = [(r, 0, PACK, nc.scalar.copy) for r in raws[:-1]]
+                parts = parts + [(raws[-1], 0, 1, nc.scalar.copy), (raws[-1], 1, PACK, nc.scalar.copy)]
+            for (raw, c0, c1), t0, t1, copy in parts:
+                copy(
+                    dealt[:, t0:t1, c0 // PACK : c1 // PACK, :].rearrange("p t m j -> p m t j"),
+                    raw[:].rearrange("p j (m t) -> p m t j", t=PACK)[:, :, t0:t1, :],
                 )
             return dealt
 
@@ -92,27 +94,29 @@ def tile_picked_edgeatt_sigmoid_po_kernel(
         x_codes = keep.tile([P, S], U32, name="x_codes", align_bytes=64)
         x_bytes = keep.tile([P, S], U8, name="x_bytes", align_bytes=64)
         nc.vector.tensor_copy(x_bytes[:], scales_all[:].indirect(offs_sb[:]))
-        for c0 in range(0, S, BANK):
-            nc.vector.tensor_copy(x_codes[:, c0 : c0 + BANK], words_all[:].indirect(entries(offs_sb, c0, BANK)))
+        nc.vector.tensor_copy(x_codes[:], words_all[:].indirect(offs_sb[:]))
 
         def product(weight, t, name, first=False):
             codes, scales = weight
-            rows = keep.tile([P, S], F32, name=f"{name}{t}")
-            for c0 in range(0, S, BANK):
+            rows = keep.tile([P, S + SPARE[name]], F32, name=f"{name}{t}")
+            if SPARE[name]:
+                nc.gpsimd.memset(rows[:, S:], 0.0)
+            if first:
+                cuts = [(0, 512, nc.scalar.copy), (512, 768, nc.vector.tensor_copy), (768, S, nc.scalar.copy)]
+            else:
+                cuts = [(0, 512, nc.scalar.copy), (512, S, nc.scalar.copy)]
+            for c0, c1, copy in cuts:
                 acc = psum.tile([P, BANK], F32, name="acc")
                 nc.tensor.matmul_mx(
-                    out=acc[:],
+                    out=acc[:, : c1 - c0],
                     lhsT=codes[:, t * P : (t + 1) * P].bitcast(FP8X4),
                     lhsT_scale=scales[:, t * P : (t + 1) * P],
-                    rhs=x_codes[:, c0 : c0 + BANK].bitcast(FP8X4),
-                    rhs_scale=x_bytes[:, c0 : c0 + BANK],
+                    rhs=x_codes[:, c0:c1].bitcast(FP8X4),
+                    rhs_scale=x_bytes[:, c0:c1],
                     start=True,
                     stop=True,
                 )
-                if first and c0 > 0:
-                    nc.vector.tensor_copy(rows[:, c0 : c0 + BANK], acc[:])
-                else:
-                    nc.scalar.copy(rows[:, c0 : c0 + BANK], acc[:])
+                copy(rows[:, c0:c1], acc[:, : c1 - c0])
             return rows
 
         y_dst = [keep.tile([P, U], F32, name=f"y_dst{t}") for t in range(PACK)]
@@ -120,14 +124,10 @@ def tile_picked_edgeatt_sigmoid_po_kernel(
         gate = [keep.tile([P, U], F32, name=f"gate{t}") for t in range(PACK)]
 
         def fetch_y(y, t):
-            for c0 in range(0, U, BANK):
-                nc.vector.tensor_copy(y_dst[t][:, c0 : c0 + BANK], y[:].indirect(entries(dst_sb, c0, BANK)))
+            nc.vector.tensor_copy(y_dst[t][:], y[:].indirect(dst_sb[:]))
 
         def add_e(e, t):
-            for c0 in range(0, U, BANK):
-                nc.vector.tensor_tensor(
-                    logit[t][:, c0 : c0 + BANK], e[:].indirect(entries(src_sb, c0, BANK)), y_dst[t][:, c0 : c0 + BANK], ADD
-                )
+            nc.vector.tensor_tensor(logit[t][:], e[:].indirect(src_sb[:]), y_dst[t][:], ADD)
 
         def squash(t, c0):
             nc.scalar.activation(gate[t][:, c0 : c0 + BANK], logit[t][:, c0 : c0 + BANK], SIGMOID)
@@ -163,6 +163,8 @@ def tile_picked_edgeatt_sigmoid_po_kernel(
         out_rows = out_0.rearrange("(p t) c -> p t c", t=PACK)
         out_words = out_1[0].rearrange("p c r -> p (c r)").bitcast(I32)
 
+        rounded = keep.tile([P, U * PACK], BF16, name="rounded", align_bytes=64)
+
         def messages(c0, n):
             msg = keep.tile([P, PACK, n], F32, name=f"msg{c0}")
             for t in range(PACK):
@@ -170,32 +172,27 @@ def tile_picked_edgeatt_sigmoid_po_kernel(
                     msg[:, t, :], h[t][:].indirect(entries(src_sb, c0, n)), gate[t][:, c0 : c0 + n], MULT
                 )
             nc.sync.dma_start(out_rows[:, :, c0 : c0 + n], msg[:])
-            rounded = keep.tile([P, n, PACK], BF16, name=f"rounded{c0}", align_bytes=64)
             copy = nc.vector.tensor_copy if c0 + n == U else nc.scalar.copy
             copy(
-                rounded[:].rearrange("p (c i) t -> p c t i", i=4),
+                rounded[:, PACK * c0 : PACK * (c0 + n)].rearrange("p (c i t) -> p c t i", i=4, t=PACK),
                 msg[:].rearrange("p t (c i) -> p c t i", i=4),
             )
-            return rounded
 
-        def planes(rounded, c0, n):
+        def planes(c0, c1, queue):
             nc.vector.quantize_mx(
-                out=out_codes[:, c0 : c0 + n].bitcast(FP8X4),
-                scales=out_scales[:, c0 : c0 + n],
-                in_=rounded[:].rearrange("p c t -> p (c t)"),
+                out=out_codes[:, c0:c1].bitcast(FP8X4),
+                scales=out_scales[:, c0:c1],
+                in_=rounded[:, PACK * c0 : PACK * c1],
             )
-            nc.sync.dma_start(out_words[:, c0 : c0 + n], out_codes[:, c0 : c0 + n].bitcast(I32))
+            queue.dma_start(out_words[:, c0:c1], out_codes[:, c0:c1].bitcast(I32))
 
-        waiting = None
-        c0 = 0
-        for n in EDGE_CHUNKS:
-            rounded = messages(c0, n)
-            if waiting is not None:
-                planes(*waiting)
-            waiting = (rounded, c0, n)
-            c0 = c0 + n
-        planes(*waiting)
+        messages(0, 512)
+        messages(512, 384)
+        planes(0, 512, nc.sync)
+        messages(896, 128)
+        planes(512, 768, nc.sync)
+        planes(768, U, nc.scalar)
         for q in range(4):
-            nc.scalar.dma_start(
+            (nc.scalar if q == 3 else nc.sync).dma_start(
                 out_2[0, 4 * q : 4 * q + 4, :].bitcast(I32), out_scales[32 * q : 32 * q + 4, :].bitcast(I32)
             )

@@ -20,7 +20,6 @@ P = 128
 PACK = 4
 BANK = 512
 LIST_ROWS = 16
-SPARE = {"y": 352, "e": 16, "h": 0}
 
 
 def tile_picked_edgeatt_sigmoid_po_kernel(
@@ -66,30 +65,30 @@ def tile_picked_edgeatt_sigmoid_po_kernel(
         table_out = keep.tile([P, 1], F32, name="table_out")
         nc.scalar.activation(table_out[:], table[:], SIGMOID)
 
-        def deal_weight(raws, name):
-            dealt = keep.tile([P, PACK, P, PACK], BF16, name=f"{name}_dealt", align_bytes=64)
-            if len(raws) == 1:
-                parts = [(raws[0], 0, PACK, nc.scalar.copy)]
-            else:
-                parts = [(r, 0, PACK, nc.scalar.copy) for r in raws[:-1]]
-                parts = parts + [(raws[-1], 0, 1, nc.scalar.copy), (raws[-1], 1, PACK, nc.scalar.copy)]
-            for (raw, c0, c1), t0, t1, copy in parts:
-                copy(
-                    dealt[:, t0:t1, c0 // PACK : c1 // PACK, :].rearrange("p t m j -> p m t j"),
-                    raw[:].rearrange("p j (m t) -> p m t j", t=PACK)[:, :, t0:t1, :],
-                )
-            return dealt
+        def deal(dealt, raw_piece, t0, t1):
+            raw, c0, c1 = raw_piece
+            nc.scalar.copy(
+                dealt[:, t0:t1, c0 // PACK : c1 // PACK, :].rearrange("p t m j -> p m t j"),
+                raw[:].rearrange("p j (m t) -> p m t j", t=PACK)[:, :, t0:t1, :],
+            )
 
-        def quantise_weight(dealt, name, cuts):
+        def mx_tiles(name):
+            dealt = keep.tile([P, PACK, P, PACK], BF16, name=f"{name}_dealt", align_bytes=64)
             codes = keep.tile([P, N], U32, name=f"{name}_codes", align_bytes=64)
             scales = keep.tile([P, N], U8, name=f"{name}_scales", align_bytes=64)
-            for t0, t1 in cuts:
-                nc.vector.quantize_mx(
-                    out=codes[:, t0 * P : t1 * P].bitcast(FP8X4),
-                    scales=scales[:, t0 * P : t1 * P],
-                    in_=dealt[:, t0:t1, :, :].rearrange("p t m j -> p (t m j)"),
-                )
-            return codes, scales
+            return dealt, codes, scales
+
+        def quantise(weight, t0, t1):
+            dealt, codes, scales = weight
+            nc.vector.quantize_mx(
+                out=codes[:, t0 * P : t1 * P].bitcast(FP8X4),
+                scales=scales[:, t0 * P : t1 * P],
+                in_=dealt[:, t0:t1, :, :].rearrange("p t m j -> p (t m j)"),
+            )
+
+        def deal_and_quantise(weight, raw_piece, t0, t1):
+            deal(weight[0], raw_piece, t0, t1)
+            quantise(weight, t0, t1)
 
         x_codes = keep.tile([P, S], U32, name="x_codes", align_bytes=64)
         x_bytes = keep.tile([P, S], U8, name="x_bytes", align_bytes=64)
@@ -97,10 +96,8 @@ def tile_picked_edgeatt_sigmoid_po_kernel(
         nc.vector.tensor_copy(x_codes[:], words_all[:].indirect(offs_sb[:]))
 
         def product(weight, t, name, first=False):
-            codes, scales = weight
-            rows = keep.tile([P, S + SPARE[name]], F32, name=f"{name}{t}")
-            if SPARE[name]:
-                nc.gpsimd.memset(rows[:, S:], 0.0)
+            codes, scales = weight[1], weight[2]
+            rows = keep.tile([P, S], F32, name=f"{name}{t}")
             if first:
                 cuts = [(0, 512, nc.scalar.copy), (512, 768, nc.vector.tensor_copy), (768, S, nc.scalar.copy)]
             else:
@@ -122,76 +119,106 @@ def tile_picked_edgeatt_sigmoid_po_kernel(
         y_dst = [keep.tile([P, U], F32, name=f"y_dst{t}") for t in range(PACK)]
         logit = [keep.tile([P, U], F32, name=f"logit{t}") for t in range(PACK)]
         gate = [keep.tile([P, U], F32, name=f"gate{t}") for t in range(PACK)]
+        HALF = U // 2
 
         def fetch_y(y, t):
-            nc.vector.tensor_copy(y_dst[t][:], y[:].indirect(dst_sb[:]))
+            for c0 in range(0, U, HALF):
+                nc.vector.tensor_copy(y_dst[t][:, c0 : c0 + HALF], y[:].indirect(entries(dst_sb, c0, HALF)))
 
         def add_e(e, t):
-            nc.vector.tensor_tensor(logit[t][:], e[:].indirect(src_sb[:]), y_dst[t][:], ADD)
+            for c0 in range(0, U, HALF):
+                nc.vector.tensor_tensor(
+                    logit[t][:, c0 : c0 + HALF],
+                    e[:].indirect(entries(src_sb, c0, HALF)),
+                    y_dst[t][:, c0 : c0 + HALF],
+                    ADD,
+                )
 
-        def squash(t, c0):
-            nc.scalar.activation(gate[t][:, c0 : c0 + BANK], logit[t][:, c0 : c0 + BANK], SIGMOID)
+        def squash(t, c0, c1):
+            nc.scalar.activation(gate[t][:, c0:c1], logit[t][:, c0:c1], SIGMOID)
 
-        w1_mx = quantise_weight(deal_weight(w1_raw, "w1"), "w1", [(0, 1), (1, 2), (2, 4)])
+        w1_mx, w2_mx, w3_mx = mx_tiles("w1"), mx_tiles("w2"), mx_tiles("w3")
+        deal(w1_mx[0], w1_raw[0], 0, PACK)
+        deal(w1_mx[0], w1_raw[1], 0, PACK)
+        deal_and_quantise(w1_mx, w1_raw[2], 0, 1)
+        deal(w1_mx[0], w1_raw[2], 1, PACK)
+        quantise(w1_mx, 1, 2)
+        quantise(w1_mx, 2, 4)
         y0 = product(w1_mx, 0, "y", first=True)
         y1 = product(w1_mx, 1, "y")
         fetch_y(y0, 0)
+        deal_and_quantise(w2_mx, w2_raw[0], 0, 2)
         y2 = product(w1_mx, 2, "y")
         fetch_y(y1, 1)
-        w2_dealt = deal_weight(w2_raw, "w2")
+        deal_and_quantise(w2_mx, w2_raw[0], 2, 4)
         y3 = product(w1_mx, 3, "y")
         fetch_y(y2, 2)
-        w2_mx = quantise_weight(w2_dealt, "w2", [(0, 4)])
         e0 = product(w2_mx, 0, "e")
         fetch_y(y3, 3)
+        deal_and_quantise(w3_mx, w3_raw[0], 0, 2)
         e1 = product(w2_mx, 1, "e")
         add_e(e0, 0)
-        w3_dealt = deal_weight(w3_raw, "w3")
+        deal_and_quantise(w3_mx, w3_raw[0], 2, 4)
         e2 = product(w2_mx, 2, "e")
         add_e(e1, 1)
-        w3_mx = quantise_weight(w3_dealt, "w3", [(0, 4)])
         e3 = product(w2_mx, 3, "e")
         add_e(e2, 2)
-        h = [product(w3_mx, t, "h") for t in range(PACK)]
         add_e(e3, 3)
-        for c0 in range(0, U, BANK):
+        stretches = [(0, 512), (512, 768), (768, 896), (896, U)]
+        h = []
+        for t in range(PACK):
+            h.append(product(w3_mx, t, "h"))
+            squash(t, *stretches[0])
+        for c0, c1 in stretches[1:]:
             for t in range(PACK):
-                squash(t, c0)
+                squash(t, c0, c1)
 
         out_codes = keep.tile([P, U], U32, name="out_codes", align_bytes=64)
         out_scales = keep.tile([P, U], U8, name="out_scales", align_bytes=64)
         out_rows = out_0.rearrange("(p t) c -> p t c", t=PACK)
         out_words = out_1[0].rearrange("p c r -> p (c r)").bitcast(I32)
 
-        rounded = keep.tile([P, U * PACK], BF16, name="rounded", align_bytes=64)
-
-        def messages(c0, n):
-            msg = keep.tile([P, PACK, n], F32, name=f"msg{c0}")
+        def messages(c0, c1, tag):
+            msg = keep.tile([P, PACK, c1 - c0], F32, name=f"msg{c0}", tag=tag, align_bytes=64)
             for t in range(PACK):
                 nc.vector.tensor_tensor(
-                    msg[:, t, :], h[t][:].indirect(entries(src_sb, c0, n)), gate[t][:, c0 : c0 + n], MULT
+                    msg[:, t, :], h[t][:].indirect(entries(src_sb, c0, c1 - c0)), gate[t][:, c0:c1], MULT
                 )
-            nc.sync.dma_start(out_rows[:, :, c0 : c0 + n], msg[:])
-            copy = nc.vector.tensor_copy if c0 + n == U else nc.scalar.copy
+            nc.sync.dma_start(out_rows[:, :, c0:c1], msg[:])
+            return msg
+
+        def rounded_tile(c0, c1, tag):
+            return keep.tile([P, (c1 - c0) * PACK], BF16, name=f"rounded{c0}", tag=tag, align_bytes=64)
+
+        def round_edges(copy, rounded, msg, a, b):
             copy(
-                rounded[:, PACK * c0 : PACK * (c0 + n)].rearrange("p (c i t) -> p c t i", i=4, t=PACK),
-                msg[:].rearrange("p t (c i) -> p c t i", i=4),
+                rounded[:, PACK * a : PACK * b].rearrange("p (c i t) -> p c t i", i=4, t=PACK),
+                msg[:, :, a:b].rearrange("p t (c i) -> p c t i", i=4),
             )
 
-        def planes(c0, c1, queue):
-            nc.vector.quantize_mx(
-                out=out_codes[:, c0:c1].bitcast(FP8X4),
-                scales=out_scales[:, c0:c1],
-                in_=rounded[:, PACK * c0 : PACK * c1],
-            )
+        def planes(rounded, c0, c1):
+            nc.vector.quantize_mx(out=out_codes[:, c0:c1].bitcast(FP8X4), scales=out_scales[:, c0:c1], in_=rounded[:])
+
+        def store_words(queue, c0, c1):
             queue.dma_start(out_words[:, c0:c1], out_codes[:, c0:c1].bitcast(I32))
 
-        messages(0, 512)
-        messages(512, 384)
-        planes(0, 512, nc.sync)
-        messages(896, 128)
-        planes(512, 768, nc.sync)
-        planes(768, U, nc.scalar)
+        rounded = []
+        for i, (c0, c1) in enumerate(stretches[:3]):
+            msg = messages(c0, c1, f"msg{i}")
+            rounded.append(rounded_tile(c0, c1, f"rounded{i}"))
+            round_edges(nc.scalar.copy, rounded[i], msg, 0, c1 - c0)
+        planes(rounded[0], *stretches[0])
+        store_words(nc.sync, *stretches[0])
+        c0, c1 = stretches[3]
+        msg = messages(c0, c1, "rounded0")
+        last = rounded_tile(c0, c1, "rounded3")
+        round_edges(nc.scalar.copy, last, msg, 0, 64)
+        planes(rounded[1], *stretches[1])
+        store_words(nc.sync, *stretches[1])
+        round_edges(nc.vector.tensor_copy, last, msg, 64, 128)
+        planes(rounded[2], *stretches[2])
+        planes(last, c0, c1)
+        store_words(nc.scalar, stretches[2][0], U)
         for q in range(4):
             (nc.scalar if q == 3 else nc.sync).dma_start(
                 out_2[0, 4 * q : 4 * q + 4, :].bitcast(I32), out_scales[32 * q : 32 * q + 4, :].bitcast(I32)

@@ -20,6 +20,7 @@ P = 128
 PACK = 4
 BANK = 512
 LIST_ROWS = 16
+SPARE = {"y": 352, "e": 16, "h": 0}
 
 
 def tile_picked_edgeatt_sigmoid_po_kernel(
@@ -47,14 +48,18 @@ def tile_picked_edgeatt_sigmoid_po_kernel(
             return raw, c0, c1
 
         nc.sync.dma_start(offs_sb[:], offs)
-        w1_raw = [load_weight(w1, "w1", 0, 128)]
+        def load_row_pair(pair):
+            raw = keep.tile([P, 2, N], F32, name=f"w1_rows{pair}")
+            nc.sync.dma_start(raw[:], w1.rearrange("(p j) c -> p j c", j=PACK)[:, 2 * pair : 2 * pair + 2, :])
+            return raw
+
+        w1_rows = [load_row_pair(0)]
         for q in range(4):
             nc.sync.dma_start(
                 scales_all[32 * q : 32 * q + 4, :].bitcast(I32), x_scales[0, 4 * q : 4 * q + 4, :].bitcast(I32)
             )
         nc.sync.dma_start(words_all[:].bitcast(I32), x_words[0].rearrange("p c r -> p (c r)").bitcast(I32))
-        w1_raw.append(load_weight(w1, "w1", 128, 320))
-        w1_raw.append(load_weight(w1, "w1", 320, 512))
+        w1_rows.append(load_row_pair(1))
         nc.sync.dma_start(dst_sb[:], dst)
         w2_raw = [load_weight(w2, "w2", 0, N)]
         nc.sync.dma_start(src_sb[:], src)
@@ -97,7 +102,9 @@ def tile_picked_edgeatt_sigmoid_po_kernel(
 
         def product(weight, t, name, first=False):
             codes, scales = weight[1], weight[2]
-            rows = keep.tile([P, S], F32, name=f"{name}{t}")
+            rows = keep.tile([P, S + SPARE[name]], F32, name=f"{name}{t}")
+            if SPARE[name]:
+                nc.vector.memset(rows[:, S:], 0.0)
             if first:
                 cuts = [(0, 512, nc.scalar.copy), (512, 768, nc.vector.tensor_copy), (768, S, nc.scalar.copy)]
             else:
@@ -119,29 +126,28 @@ def tile_picked_edgeatt_sigmoid_po_kernel(
         y_dst = [keep.tile([P, U], F32, name=f"y_dst{t}") for t in range(PACK)]
         logit = [keep.tile([P, U], F32, name=f"logit{t}") for t in range(PACK)]
         gate = [keep.tile([P, U], F32, name=f"gate{t}") for t in range(PACK)]
-        HALF = U // 2
 
         def fetch_y(y, t):
-            for c0 in range(0, U, HALF):
-                nc.vector.tensor_copy(y_dst[t][:, c0 : c0 + HALF], y[:].indirect(entries(dst_sb, c0, HALF)))
+            nc.vector.tensor_copy(y_dst[t][:], y[:].indirect(dst_sb[:]))
 
         def add_e(e, t):
-            for c0 in range(0, U, HALF):
-                nc.vector.tensor_tensor(
-                    logit[t][:, c0 : c0 + HALF],
-                    e[:].indirect(entries(src_sb, c0, HALF)),
-                    y_dst[t][:, c0 : c0 + HALF],
-                    ADD,
-                )
+            nc.vector.tensor_tensor(logit[t][:], e[:].indirect(src_sb[:]), y_dst[t][:], ADD)
 
         def squash(t, c0, c1):
             nc.scalar.activation(gate[t][:, c0:c1], logit[t][:, c0:c1], SIGMOID)
 
         w1_mx, w2_mx, w3_mx = mx_tiles("w1"), mx_tiles("w2"), mx_tiles("w3")
-        deal(w1_mx[0], w1_raw[0], 0, PACK)
-        deal(w1_mx[0], w1_raw[1], 0, PACK)
-        deal_and_quantise(w1_mx, w1_raw[2], 0, 1)
-        deal(w1_mx[0], w1_raw[2], 1, PACK)
+
+        def deal_rows(pair, t0, t1):
+            nc.scalar.copy(
+                w1_mx[0][:, t0:t1, :, 2 * pair : 2 * pair + 2].rearrange("p t m j -> p m t j"),
+                w1_rows[pair][:].rearrange("p j (m t) -> p m t j", t=PACK)[:, :, t0:t1, :],
+            )
+
+        deal_rows(0, 0, PACK)
+        deal_rows(1, 0, 1)
+        quantise(w1_mx, 0, 1)
+        deal_rows(1, 1, PACK)
         quantise(w1_mx, 1, 2)
         quantise(w1_mx, 2, 4)
         y0 = product(w1_mx, 0, "y", first=True)

@@ -170,61 +170,75 @@ def tile_picked_edgeatt_sigmoid_po_kernel(
         e3 = product(w2_mx, 3, "e")
         add_e(e2, 2)
         add_e(e3, 3)
-        stretches = [(0, 512), (512, 768), (768, 896), (896, U)]
+        stretches = [(0, 256), (256, 512), (512, 768), (768, 896), (896, U)]
         h = []
         for t in range(PACK):
             h.append(product(w3_mx, t, "h"))
             squash(t, *stretches[0])
-        for c0, c1 in stretches[1:]:
-            for t in range(PACK):
-                squash(t, c0, c1)
 
         out_codes = keep.tile([P, U], U32, name="out_codes", align_bytes=64)
         out_scales = keep.tile([P, U], U8, name="out_scales", align_bytes=64)
+        rounded = keep.tile([P, U * PACK], BF16, name="rounded", align_bytes=64)
         out_rows = out_0.rearrange("(p t) c -> p t c", t=PACK)
         out_words = out_1[0].rearrange("p c r -> p (c r)").bitcast(I32)
+        stores = [(0, 512), (512, 768), (768, 896), (896, U)]
+        msgs = [keep.tile([P, PACK, c1 - c0], F32, name=f"msg{c0}") for c0, c1 in stores]
 
-        def messages(c0, c1, tag):
-            msg = keep.tile([P, PACK, c1 - c0], F32, name=f"msg{c0}", tag=tag, align_bytes=64)
+        def msg_view(c0, c1):
+            i = max(k for k in range(len(stores)) if stores[k][0] <= c0)
+            return msgs[i][:, :, c0 - stores[i][0] : c1 - stores[i][0]]
+
+        def squash_all(c0, c1):
+            for t in range(PACK):
+                squash(t, c0, c1)
+
+        def messages(c0, c1):
             for t in range(PACK):
                 nc.vector.tensor_tensor(
-                    msg[:, t, :], h[t][:].indirect(entries(src_sb, c0, c1 - c0)), gate[t][:, c0:c1], MULT
+                    msg_view(c0, c1)[:, t, :], h[t][:].indirect(entries(src_sb, c0, c1 - c0)), gate[t][:, c0:c1], MULT
                 )
-            nc.sync.dma_start(out_rows[:, :, c0:c1], msg[:])
-            return msg
+            for (s0, s1), msg in zip(stores, msgs):
+                if s1 == c1:
+                    nc.sync.dma_start(out_rows[:, :, s0:s1], msg[:])
 
-        def rounded_tile(c0, c1, tag):
-            return keep.tile([P, (c1 - c0) * PACK], BF16, name=f"rounded{c0}", tag=tag, align_bytes=64)
-
-        def round_edges(copy, rounded, msg, a, b):
+        def round_edges(copy, c0, c1):
             copy(
-                rounded[:, PACK * a : PACK * b].rearrange("p (c i t) -> p c t i", i=4, t=PACK),
-                msg[:, :, a:b].rearrange("p t (c i) -> p c t i", i=4),
+                rounded[:, PACK * c0 : PACK * c1].rearrange("p (c i t) -> p c t i", i=4, t=PACK),
+                msg_view(c0, c1).rearrange("p t (c i) -> p c t i", i=4),
             )
 
-        def planes(rounded, c0, c1):
-            nc.vector.quantize_mx(out=out_codes[:, c0:c1].bitcast(FP8X4), scales=out_scales[:, c0:c1], in_=rounded[:])
+        def planes(c0, c1):
+            nc.vector.quantize_mx(
+                out=out_codes[:, c0:c1].bitcast(FP8X4),
+                scales=out_scales[:, c0:c1],
+                in_=rounded[:, PACK * c0 : PACK * c1],
+            )
 
         def store_words(queue, c0, c1):
             queue.dma_start(out_words[:, c0:c1], out_codes[:, c0:c1].bitcast(I32))
 
-        rounded = []
-        for i, (c0, c1) in enumerate(stretches[:3]):
-            msg = messages(c0, c1, f"msg{i}")
-            rounded.append(rounded_tile(c0, c1, f"rounded{i}"))
-            round_edges(nc.scalar.copy, rounded[i], msg, 0, c1 - c0)
-        planes(rounded[0], *stretches[0])
-        store_words(nc.sync, *stretches[0])
-        c0, c1 = stretches[3]
-        msg = messages(c0, c1, "rounded0")
-        last = rounded_tile(c0, c1, "rounded3")
-        round_edges(nc.scalar.copy, last, msg, 0, 64)
-        planes(rounded[1], *stretches[1])
-        store_words(nc.sync, *stretches[1])
-        round_edges(nc.vector.tensor_copy, last, msg, 64, 128)
-        planes(rounded[2], *stretches[2])
-        planes(last, c0, c1)
-        store_words(nc.scalar, stretches[2][0], U)
+        squash_all(*stretches[1])
+        squash_all(*stretches[2])
+        messages(*stretches[0])
+        round_edges(nc.scalar.copy, *stretches[0])
+        squash_all(*stretches[3])
+        messages(*stretches[1])
+        round_edges(nc.scalar.copy, *stretches[1])
+        squash_all(*stretches[4])
+        messages(*stretches[2])
+        round_edges(nc.scalar.copy, *stretches[2])
+        messages(*stretches[3])
+        round_edges(nc.scalar.copy, *stretches[3])
+        planes(0, 512)
+        store_words(nc.sync, 0, 512)
+        messages(*stretches[4])
+        round_edges(nc.scalar.copy, 896, 960)
+        planes(512, 768)
+        store_words(nc.sync, 512, 768)
+        round_edges(nc.vector.tensor_copy, 960, U)
+        planes(768, 896)
+        planes(896, U)
+        store_words(nc.scalar, 768, U)
         for q in range(4):
             (nc.scalar if q == 3 else nc.sync).dma_start(
                 out_2[0, 4 * q : 4 * q + 4, :].bitcast(I32), out_scales[32 * q : 32 * q + 4, :].bitcast(I32)

@@ -20,7 +20,15 @@ P = 128
 PACK = 4
 BANK = 512
 LIST_ROWS = 16
+QUADRANTS = 4
+
 SPARE = {"y": 352, "e": 16, "h": 0}
+
+W1_PIECES = [(0, 128), (128, 320), (320, N)]
+
+STRETCHES = [(0, 256), (256, 512), (512, 768), (768, 896), (896, U)]
+STORES = [(0, 512), (512, 768), (768, 896), (896, U)]
+LAST_SPLIT = 960
 
 
 def tile_picked_edgeatt_sigmoid_po_kernel(
@@ -48,40 +56,35 @@ def tile_picked_edgeatt_sigmoid_po_kernel(
             return raw, c0, c1
 
         nc.sync.dma_start(offs_sb[:], offs)
-        def load_row_pair(pair):
-            raw = keep.tile([P, 2, N], F32, name=f"w1_rows{pair}")
-            nc.sync.dma_start(raw[:], w1.rearrange("(p j) c -> p j c", j=PACK)[:, 2 * pair : 2 * pair + 2, :])
-            return raw
-
-        w1_rows = [load_row_pair(0)]
-        for q in range(4):
+        w1_raw = [load_weight(w1, "w1", *W1_PIECES[0])]
+        for q in range(QUADRANTS):
             nc.sync.dma_start(
                 scales_all[32 * q : 32 * q + 4, :].bitcast(I32), x_scales[0, 4 * q : 4 * q + 4, :].bitcast(I32)
             )
         nc.sync.dma_start(words_all[:].bitcast(I32), x_words[0].rearrange("p c r -> p (c r)").bitcast(I32))
-        w1_rows.append(load_row_pair(1))
+        w1_raw.extend(load_weight(w1, "w1", c0, c1) for c0, c1 in W1_PIECES[1:])
         nc.sync.dma_start(dst_sb[:], dst)
-        w2_raw = [load_weight(w2, "w2", 0, N)]
+        w2_raw = load_weight(w2, "w2", 0, N)
         nc.sync.dma_start(src_sb[:], src)
-        w3_raw = [load_weight(w3, "w3", 0, N)]
+        w3_raw = load_weight(w3, "w3", 0, N)
 
         table = keep.tile([P, 1], F32, name="table")
         nc.gpsimd.memset(table[:], 0.0)
         table_out = keep.tile([P, 1], F32, name="table_out")
         nc.scalar.activation(table_out[:], table[:], SIGMOID)
 
-        def deal(dealt, raw_piece, t0, t1):
-            raw, c0, c1 = raw_piece
-            nc.scalar.copy(
-                dealt[:, t0:t1, c0 // PACK : c1 // PACK, :].rearrange("p t m j -> p m t j"),
-                raw[:].rearrange("p j (m t) -> p m t j", t=PACK)[:, :, t0:t1, :],
-            )
-
         def mx_tiles(name):
             dealt = keep.tile([P, PACK, P, PACK], BF16, name=f"{name}_dealt", align_bytes=64)
             codes = keep.tile([P, N], U32, name=f"{name}_codes", align_bytes=64)
             scales = keep.tile([P, N], U8, name=f"{name}_scales", align_bytes=64)
             return dealt, codes, scales
+
+        def deal(weight, piece, t0, t1):
+            raw, c0, c1 = piece
+            nc.scalar.copy(
+                weight[0][:, t0:t1, c0 // PACK : c1 // PACK, :].rearrange("p t m j -> p m t j"),
+                raw[:].rearrange("p j (m t) -> p m t j", t=PACK)[:, :, t0:t1, :],
+            )
 
         def quantise(weight, t0, t1):
             dealt, codes, scales = weight
@@ -91,8 +94,8 @@ def tile_picked_edgeatt_sigmoid_po_kernel(
                 in_=dealt[:, t0:t1, :, :].rearrange("p t m j -> p (t m j)"),
             )
 
-        def deal_and_quantise(weight, raw_piece, t0, t1):
-            deal(weight[0], raw_piece, t0, t1)
+        def deal_and_quantise(weight, piece, t0, t1):
+            deal(weight, piece, t0, t1)
             quantise(weight, t0, t1)
 
         x_codes = keep.tile([P, S], U32, name="x_codes", align_bytes=64)
@@ -100,15 +103,14 @@ def tile_picked_edgeatt_sigmoid_po_kernel(
         nc.vector.tensor_copy(x_bytes[:], scales_all[:].indirect(offs_sb[:]))
         nc.vector.tensor_copy(x_codes[:], words_all[:].indirect(offs_sb[:]))
 
-        def product(weight, t, name, first=False):
+        by_banks = [(0, BANK, nc.scalar.copy), (BANK, S, nc.scalar.copy)]
+        shared = [(0, BANK, nc.scalar.copy), (BANK, 768, nc.vector.tensor_copy), (768, S, nc.scalar.copy)]
+
+        def product(weight, t, name, cuts):
             codes, scales = weight[1], weight[2]
             rows = keep.tile([P, S + SPARE[name]], F32, name=f"{name}{t}")
             if SPARE[name]:
                 nc.vector.memset(rows[:, S:], 0.0)
-            if first:
-                cuts = [(0, 512, nc.scalar.copy), (512, 768, nc.vector.tensor_copy), (768, S, nc.scalar.copy)]
-            else:
-                cuts = [(0, 512, nc.scalar.copy), (512, S, nc.scalar.copy)]
             for c0, c1, copy in cuts:
                 acc = psum.tile([P, BANK], F32, name="acc")
                 nc.tensor.matmul_mx(
@@ -138,57 +140,51 @@ def tile_picked_edgeatt_sigmoid_po_kernel(
 
         w1_mx, w2_mx, w3_mx = mx_tiles("w1"), mx_tiles("w2"), mx_tiles("w3")
 
-        def deal_rows(pair, t0, t1):
-            nc.scalar.copy(
-                w1_mx[0][:, t0:t1, :, 2 * pair : 2 * pair + 2].rearrange("p t m j -> p m t j"),
-                w1_rows[pair][:].rearrange("p j (m t) -> p m t j", t=PACK)[:, :, t0:t1, :],
-            )
-
-        deal_rows(0, 0, PACK)
-        deal_rows(1, 0, 1)
-        quantise(w1_mx, 0, 1)
-        deal_rows(1, 1, PACK)
+        for piece in w1_raw[:-1]:
+            deal(w1_mx, piece, 0, PACK)
+        deal_and_quantise(w1_mx, w1_raw[-1], 0, 1)
+        deal(w1_mx, w1_raw[-1], 1, PACK)
         quantise(w1_mx, 1, 2)
-        quantise(w1_mx, 2, 4)
-        y0 = product(w1_mx, 0, "y", first=True)
-        y1 = product(w1_mx, 1, "y")
+        quantise(w1_mx, 2, PACK)
+
+        y0 = product(w1_mx, 0, "y", shared)
+        y1 = product(w1_mx, 1, "y", by_banks)
         fetch_y(y0, 0)
-        deal_and_quantise(w2_mx, w2_raw[0], 0, 2)
-        y2 = product(w1_mx, 2, "y")
+        deal_and_quantise(w2_mx, w2_raw, 0, 2)
+        y2 = product(w1_mx, 2, "y", by_banks)
         fetch_y(y1, 1)
-        deal_and_quantise(w2_mx, w2_raw[0], 2, 4)
-        y3 = product(w1_mx, 3, "y")
+        deal_and_quantise(w2_mx, w2_raw, 2, PACK)
+        y3 = product(w1_mx, 3, "y", by_banks)
         fetch_y(y2, 2)
-        e0 = product(w2_mx, 0, "e")
+        e0 = product(w2_mx, 0, "e", by_banks)
         fetch_y(y3, 3)
-        deal_and_quantise(w3_mx, w3_raw[0], 0, 2)
-        e1 = product(w2_mx, 1, "e")
+        deal_and_quantise(w3_mx, w3_raw, 0, 2)
+        e1 = product(w2_mx, 1, "e", by_banks)
         add_e(e0, 0)
-        deal_and_quantise(w3_mx, w3_raw[0], 2, 4)
-        e2 = product(w2_mx, 2, "e")
+        deal_and_quantise(w3_mx, w3_raw, 2, PACK)
+        e2 = product(w2_mx, 2, "e", by_banks)
         add_e(e1, 1)
-        e3 = product(w2_mx, 3, "e")
+        e3 = product(w2_mx, 3, "e", by_banks)
         add_e(e2, 2)
         add_e(e3, 3)
-        stretches = [(0, 256), (256, 512), (512, 768), (768, 896), (896, U)]
+
         h = []
         for t in range(PACK):
-            h.append(product(w3_mx, t, "h"))
-            squash(t, *stretches[0])
+            h.append(product(w3_mx, t, "h", by_banks))
+            squash(t, *STRETCHES[0])
 
         out_codes = keep.tile([P, U], U32, name="out_codes", align_bytes=64)
         out_scales = keep.tile([P, U], U8, name="out_scales", align_bytes=64)
         rounded = keep.tile([P, U * PACK], BF16, name="rounded", align_bytes=64)
         out_rows = out_0.rearrange("(p t) c -> p t c", t=PACK)
         out_words = out_1[0].rearrange("p c r -> p (c r)").bitcast(I32)
-        stores = [(0, 512), (512, 768), (768, 896), (896, U)]
-        msgs = [keep.tile([P, PACK, c1 - c0], F32, name=f"msg{c0}") for c0, c1 in stores]
+        msgs = [keep.tile([P, PACK, c1 - c0], F32, name=f"msg{c0}") for c0, c1 in STORES]
 
         def msg_view(c0, c1):
-            i = max(k for k in range(len(stores)) if stores[k][0] <= c0)
-            return msgs[i][:, :, c0 - stores[i][0] : c1 - stores[i][0]]
+            i = max(k for k in range(len(STORES)) if STORES[k][0] <= c0)
+            return msgs[i][:, :, c0 - STORES[i][0] : c1 - STORES[i][0]]
 
-        def squash_all(c0, c1):
+        def gates(c0, c1):
             for t in range(PACK):
                 squash(t, c0, c1)
 
@@ -197,7 +193,7 @@ def tile_picked_edgeatt_sigmoid_po_kernel(
                 nc.vector.tensor_tensor(
                     msg_view(c0, c1)[:, t, :], h[t][:].indirect(entries(src_sb, c0, c1 - c0)), gate[t][:, c0:c1], MULT
                 )
-            for (s0, s1), msg in zip(stores, msgs):
+            for (s0, s1), msg in zip(STORES, msgs):
                 if s1 == c1:
                     nc.sync.dma_start(out_rows[:, :, s0:s1], msg[:])
 
@@ -217,29 +213,27 @@ def tile_picked_edgeatt_sigmoid_po_kernel(
         def store_words(queue, c0, c1):
             queue.dma_start(out_words[:, c0:c1], out_codes[:, c0:c1].bitcast(I32))
 
-        squash_all(*stretches[1])
-        squash_all(*stretches[2])
-        messages(*stretches[0])
-        round_edges(nc.scalar.copy, *stretches[0])
-        squash_all(*stretches[3])
-        messages(*stretches[1])
-        round_edges(nc.scalar.copy, *stretches[1])
-        squash_all(*stretches[4])
-        messages(*stretches[2])
-        round_edges(nc.scalar.copy, *stretches[2])
-        messages(*stretches[3])
-        round_edges(nc.scalar.copy, *stretches[3])
-        planes(0, 512)
-        store_words(nc.sync, 0, 512)
-        messages(*stretches[4])
-        round_edges(nc.scalar.copy, 896, 960)
-        planes(512, 768)
-        store_words(nc.sync, 512, 768)
-        round_edges(nc.vector.tensor_copy, 960, U)
-        planes(768, 896)
-        planes(896, U)
-        store_words(nc.scalar, 768, U)
-        for q in range(4):
-            (nc.scalar if q == 3 else nc.sync).dma_start(
+        ahead = 3
+        for c0, c1 in STRETCHES[1:ahead]:
+            gates(c0, c1)
+        for i, (c0, c1) in enumerate(STRETCHES[:-1]):
+            messages(c0, c1)
+            round_edges(nc.scalar.copy, c0, c1)
+            if i + ahead < len(STRETCHES):
+                gates(*STRETCHES[i + ahead])
+
+        planes(*STORES[0])
+        store_words(nc.sync, *STORES[0])
+        messages(*STRETCHES[-1])
+        round_edges(nc.scalar.copy, STRETCHES[-1][0], LAST_SPLIT)
+        planes(*STORES[1])
+        store_words(nc.sync, *STORES[1])
+        round_edges(nc.vector.tensor_copy, LAST_SPLIT, U)
+        planes(*STORES[2])
+        planes(*STORES[3])
+        store_words(nc.scalar, STORES[2][0], U)
+        for q in range(QUADRANTS):
+            queue = nc.scalar if q == QUADRANTS - 1 else nc.sync
+            queue.dma_start(
                 out_2[0, 4 * q : 4 * q + 4, :].bitcast(I32), out_scales[32 * q : 32 * q + 4, :].bitcast(I32)
             )

@@ -15,6 +15,7 @@ FP8X4 = mybir.dt.float8_e4m3fn_x4
 ADD = mybir.AluOpType.add
 MULT = mybir.AluOpType.mult
 SIGMOID = mybir.ActivationFunctionType.Sigmoid
+COPY = mybir.ActivationFunctionType.Copy
 
 P = 128
 PACK = 4
@@ -22,11 +23,11 @@ BANK = 512
 LIST_ROWS = 16
 QUADRANTS = 4
 
-SPARE = {"y": 352, "e": 16, "h": 0}
+SPARE = {"y": 16, "e": 16, "h": 0}
 
 W1_PIECES = [(0, 128), (128, 320), (320, N)]
 
-STRETCHES = [(0, 256), (256, 512), (512, 768), (768, 896), (896, U)]
+STRETCHES = [(0, 512), (512, 768), (768, 896), (896, U)]
 STORES = [(0, 512), (512, 768), (768, 896), (896, U)]
 LAST_SPLIT = 960
 
@@ -74,14 +75,14 @@ def tile_picked_edgeatt_sigmoid_po_kernel(
         nc.scalar.activation(table_out[:], table[:], SIGMOID)
 
         def mx_tiles(name):
-            dealt = keep.tile([P, PACK, P, PACK], BF16, name=f"{name}_dealt", align_bytes=64)
+            dealt = keep.tile([P, PACK, P, PACK], BF16, name="dealt", align_bytes=64)
             codes = keep.tile([P, N], U32, name=f"{name}_codes", align_bytes=64)
             scales = keep.tile([P, N], U8, name=f"{name}_scales", align_bytes=64)
             return dealt, codes, scales
 
-        def deal(weight, piece, t0, t1):
+        def deal(weight, piece, t0, t1, copy=nc.scalar.copy):
             raw, c0, c1 = piece
-            nc.scalar.copy(
+            copy(
                 weight[0][:, t0:t1, c0 // PACK : c1 // PACK, :].rearrange("p t m j -> p m t j"),
                 raw[:].rearrange("p j (m t) -> p m t j", t=PACK)[:, :, t0:t1, :],
             )
@@ -94,21 +95,18 @@ def tile_picked_edgeatt_sigmoid_po_kernel(
                 in_=dealt[:, t0:t1, :, :].rearrange("p t m j -> p (t m j)"),
             )
 
-        def deal_and_quantise(weight, piece, t0, t1):
-            deal(weight, piece, t0, t1)
-            quantise(weight, t0, t1)
-
         x_codes = keep.tile([P, S], U32, name="x_codes", align_bytes=64)
         x_bytes = keep.tile([P, S], U8, name="x_bytes", align_bytes=64)
         nc.vector.tensor_copy(x_bytes[:], scales_all[:].indirect(offs_sb[:]))
         nc.vector.tensor_copy(x_codes[:], words_all[:].indirect(offs_sb[:]))
 
         by_banks = [(0, BANK, nc.scalar.copy), (BANK, S, nc.scalar.copy)]
-        shared = [(0, BANK, nc.scalar.copy), (BANK, 768, nc.vector.tensor_copy), (768, S, nc.scalar.copy)]
+        shared = [(0, BANK, nc.scalar.copy), (BANK, S, nc.vector.tensor_copy)]
+        by_vector = [(0, BANK, nc.vector.tensor_copy), (BANK, S, nc.vector.tensor_copy)]
 
-        def product(weight, t, name, cuts):
+        def product(weight, t, name, cuts, tag=None):
             codes, scales = weight[1], weight[2]
-            rows = keep.tile([P, S + SPARE[name]], F32, name=f"{name}{t}")
+            rows = keep.tile([P, S + SPARE[name]], F32, name=tag or f"{name}{t}")
             if SPARE[name]:
                 nc.vector.memset(rows[:, S:], 0.0)
             for c0, c1, copy in cuts:
@@ -125,12 +123,12 @@ def tile_picked_edgeatt_sigmoid_po_kernel(
                 copy(rows[:, c0:c1], acc[:, : c1 - c0])
             return rows
 
-        y_dst = [keep.tile([P, U], F32, name=f"y_dst{t}") for t in range(PACK)]
+        y_dst = [keep.tile([P, U], F32, name="y_dst", bufs=PACK - 1) for t in range(PACK)]
         logit = [keep.tile([P, U], F32, name=f"logit{t}") for t in range(PACK)]
         gate = [keep.tile([P, U], F32, name=f"gate{t}") for t in range(PACK)]
 
         def fetch_y(y, t):
-            nc.vector.tensor_copy(y_dst[t][:], y[:].indirect(dst_sb[:]))
+            nc.scalar.activation(y_dst[t][:], y[:].indirect(dst_sb[:]), COPY)
 
         def add_e(e, t):
             nc.vector.tensor_tensor(logit[t][:], e[:].indirect(src_sb[:]), y_dst[t][:], ADD)
@@ -138,35 +136,29 @@ def tile_picked_edgeatt_sigmoid_po_kernel(
         def squash(t, c0, c1):
             nc.scalar.activation(gate[t][:, c0:c1], logit[t][:, c0:c1], SIGMOID)
 
-        w1_mx, w2_mx, w3_mx = mx_tiles("w1"), mx_tiles("w2"), mx_tiles("w3")
+        w1_mx = mx_tiles("w1")
 
         for piece in w1_raw[:-1]:
             deal(w1_mx, piece, 0, PACK)
-        deal_and_quantise(w1_mx, w1_raw[-1], 0, 1)
+        deal(w1_mx, w1_raw[-1], 0, 1)
+        quantise(w1_mx, 0, 1)
         deal(w1_mx, w1_raw[-1], 1, PACK)
         quantise(w1_mx, 1, 2)
         quantise(w1_mx, 2, PACK)
 
-        y0 = product(w1_mx, 0, "y", shared)
-        y1 = product(w1_mx, 1, "y", by_banks)
-        fetch_y(y0, 0)
-        deal_and_quantise(w2_mx, w2_raw, 0, 2)
-        y2 = product(w1_mx, 2, "y", by_banks)
-        fetch_y(y1, 1)
-        deal_and_quantise(w2_mx, w2_raw, 2, PACK)
-        y3 = product(w1_mx, 3, "y", by_banks)
-        fetch_y(y2, 2)
-        e0 = product(w2_mx, 0, "e", by_banks)
-        fetch_y(y3, 3)
-        deal_and_quantise(w3_mx, w3_raw, 0, 2)
-        e1 = product(w2_mx, 1, "e", by_banks)
-        add_e(e0, 0)
-        deal_and_quantise(w3_mx, w3_raw, 2, PACK)
-        e2 = product(w2_mx, 2, "e", by_banks)
-        add_e(e1, 1)
-        e3 = product(w2_mx, 3, "e", by_banks)
-        add_e(e2, 2)
-        add_e(e3, 3)
+        w2_mx = mx_tiles("w2")
+        deal(w2_mx, w2_raw, 0, PACK, nc.gpsimd.tensor_copy)
+        for t in range(PACK - 1):
+            fetch_y(product(w1_mx, t, "y", by_vector if t else shared), t)
+        quantise(w2_mx, 0, PACK)
+        fetch_y(product(w1_mx, PACK - 1, "y", by_vector, tag="w2_raw0"), PACK - 1)
+        w3_mx = mx_tiles("w3")
+        deal(w3_mx, w3_raw, 0, PACK, nc.gpsimd.tensor_copy)
+        e = [product(w2_mx, t, "e", by_vector) for t in range(1)]
+        quantise(w3_mx, 0, PACK)
+        e.extend(product(w2_mx, t, "e", by_banks) for t in range(1, PACK))
+        for t in range(PACK):
+            add_e(e[t], t)
 
         h = []
         for t in range(PACK):

@@ -154,9 +154,9 @@ def tile_picked_edgeatt_sigmoid_po_kernel(
         fetch_y(product(w1_mx, PACK - 1, "y", by_vector, tag="w2_raw0"), PACK - 1)
         w3_mx = mx_tiles("w3")
         deal(w3_mx, w3_raw, 0, PACK, nc.gpsimd.tensor_copy)
-        e = [product(w2_mx, t, "e", by_vector) for t in range(1)]
+        e = [product(w2_mx, t, "e", by_vector) for t in range(2)]
         quantise(w3_mx, 0, PACK)
-        e.extend(product(w2_mx, t, "e", by_banks) for t in range(1, PACK))
+        e.extend(product(w2_mx, t, "e", by_banks) for t in range(2, PACK))
         for t in range(PACK):
             add_e(e[t], t)
 

@@ -27,9 +27,10 @@ SPARE = {"y": 16, "e": 16, "h": 0}
 
 W1_PIECES = [(0, 128), (128, 320), (320, N)]
 
-STRETCHES = [(0, 512), (512, 768), (768, 896), (896, U)]
-STORES = [(0, 512), (512, 768), (768, 896), (896, U)]
-LAST_SPLIT = 960
+STRETCHES = [(0, 256), (256, 512), (512, 768), (768, U)]
+LAST_SPLIT = 832
+LONG = 3
+STORES = [(0, 512), (512, 768), (768, U)]
 
 
 def tile_picked_edgeatt_sigmoid_po_kernel(
@@ -101,7 +102,7 @@ def tile_picked_edgeatt_sigmoid_po_kernel(
         nc.vector.tensor_copy(x_codes[:], words_all[:].indirect(offs_sb[:]))
 
         by_banks = [(0, BANK, nc.scalar.copy), (BANK, S, nc.scalar.copy)]
-        shared = [(0, BANK, nc.scalar.copy), (BANK, S, nc.vector.tensor_copy)]
+        shared = [(0, BANK, nc.scalar.copy), (BANK, 768, nc.vector.tensor_copy), (768, S, nc.scalar.copy)]
         by_vector = [(0, BANK, nc.vector.tensor_copy), (BANK, S, nc.vector.tensor_copy)]
 
         def product(weight, t, name, cuts, tag=None):
@@ -124,17 +125,17 @@ def tile_picked_edgeatt_sigmoid_po_kernel(
             return rows
 
         y_dst = [keep.tile([P, U], F32, name="y_dst", bufs=PACK - 1) for t in range(PACK)]
-        logit = [keep.tile([P, U], F32, name=f"logit{t}") for t in range(PACK)]
-        gate = [keep.tile([P, U], F32, name=f"gate{t}") for t in range(PACK)]
+        logit = keep.tile([P, PACK, U], F32, name="logit")
+        gate = keep.tile([P, PACK, U], F32, name="gate")
 
         def fetch_y(y, t):
             nc.scalar.activation(y_dst[t][:], y[:].indirect(dst_sb[:]), COPY)
 
         def add_e(e, t):
-            nc.vector.tensor_tensor(logit[t][:], e[:].indirect(src_sb[:]), y_dst[t][:], ADD)
+            nc.vector.tensor_tensor(logit[:, t, :], e[:].indirect(src_sb[:]), y_dst[t][:], ADD)
 
-        def squash(t, c0, c1):
-            nc.scalar.activation(gate[t][:, c0:c1], logit[t][:, c0:c1], SIGMOID)
+        def squash(t0, t1, c0, c1):
+            nc.scalar.activation(gate[:, t0:t1, c0:c1], logit[:, t0:t1, c0:c1], SIGMOID)
 
         w1_mx = mx_tiles("w1")
 
@@ -160,39 +161,36 @@ def tile_picked_edgeatt_sigmoid_po_kernel(
         for t in range(PACK):
             add_e(e[t], t)
 
+        wide = STRETCHES[LONG][0]
         h = []
         for t in range(PACK):
             h.append(product(w3_mx, t, "h", by_banks))
-            squash(t, *STRETCHES[0])
+            squash(t, t + 1, 0, wide if t < PACK - 1 else STRETCHES[0][1])
+        squash(PACK - 1, PACK, STRETCHES[0][1], wide)
 
         out_codes = keep.tile([P, U], U32, name="out_codes", align_bytes=64)
         out_scales = keep.tile([P, U], U8, name="out_scales", align_bytes=64)
         rounded = keep.tile([P, U * PACK], BF16, name="rounded", align_bytes=64)
         out_rows = out_0.rearrange("(p t) c -> p t c", t=PACK)
         out_words = out_1[0].rearrange("p c r -> p (c r)").bitcast(I32)
-        msgs = [keep.tile([P, PACK, c1 - c0], F32, name=f"msg{c0}") for c0, c1 in STORES]
-
-        def msg_view(c0, c1):
-            i = max(k for k in range(len(STORES)) if STORES[k][0] <= c0)
-            return msgs[i][:, :, c0 - STORES[i][0] : c1 - STORES[i][0]]
+        msg = keep.tile([P, PACK, U], F32, name="msg")
 
         def gates(c0, c1):
-            for t in range(PACK):
-                squash(t, c0, c1)
+            squash(0, PACK, c0, c1)
 
-        def messages(c0, c1):
-            for t in range(PACK):
+        def messages(tiles, c0, c1):
+            for t in tiles:
                 nc.vector.tensor_tensor(
-                    msg_view(c0, c1)[:, t, :], h[t][:].indirect(entries(src_sb, c0, c1 - c0)), gate[t][:, c0:c1], MULT
+                    msg[:, t, c0:c1], h[t][:].indirect(entries(src_sb, c0, c1 - c0)), gate[:, t, c0:c1], MULT
                 )
-            for (s0, s1), msg in zip(STORES, msgs):
-                if s1 == c1:
-                    nc.sync.dma_start(out_rows[:, :, s0:s1], msg[:])
+
+        def store_rows(t0, t1, c0, c1):
+            nc.sync.dma_start(out_rows[:, t0:t1, c0:c1], msg[:, t0:t1, c0:c1])
 
         def round_edges(copy, c0, c1):
             copy(
                 rounded[:, PACK * c0 : PACK * c1].rearrange("p (c i t) -> p c t i", i=4, t=PACK),
-                msg_view(c0, c1).rearrange("p t (c i) -> p c t i", i=4),
+                msg[:, :, c0:c1].rearrange("p t (c i) -> p c t i", i=4),
             )
 
         def planes(c0, c1):
@@ -205,24 +203,25 @@ def tile_picked_edgeatt_sigmoid_po_kernel(
         def store_words(queue, c0, c1):
             queue.dma_start(out_words[:, c0:c1], out_codes[:, c0:c1].bitcast(I32))
 
-        ahead = 3
-        for c0, c1 in STRETCHES[1:ahead]:
-            gates(c0, c1)
-        for i, (c0, c1) in enumerate(STRETCHES[:-1]):
-            messages(c0, c1)
+        messages([0, 1], 0, wide)
+        store_rows(0, 2, 0, wide)
+        messages([2], 0, wide)
+        for c0, c1 in STRETCHES[:LONG]:
+            messages([PACK - 1], c0, c1)
+        store_rows(2, PACK, 0, wide)
+        gates(*STRETCHES[3])
+        for t in (0, 2):
+            messages([t, t + 1], wide, U)
+            store_rows(t, t + 2, wide, U)
+        for c0, c1 in STRETCHES[:LONG]:
             round_edges(nc.scalar.copy, c0, c1)
-            if i + ahead < len(STRETCHES):
-                gates(*STRETCHES[i + ahead])
-
+        round_edges(nc.scalar.copy, wide, LAST_SPLIT)
         planes(*STORES[0])
         store_words(nc.sync, *STORES[0])
-        messages(*STRETCHES[-1])
-        round_edges(nc.scalar.copy, STRETCHES[-1][0], LAST_SPLIT)
+        round_edges(nc.vector.tensor_copy, LAST_SPLIT, U)
         planes(*STORES[1])
         store_words(nc.sync, *STORES[1])
-        round_edges(nc.vector.tensor_copy, LAST_SPLIT, U)
-        planes(*STORES[2])
-        planes(*STORES[3])
+        planes(STORES[2][0], U)
         store_words(nc.scalar, STORES[2][0], U)
         for q in range(QUADRANTS):
             queue = nc.scalar if q == QUADRANTS - 1 else nc.sync

@@ -28,7 +28,7 @@ SPARE = {"y": 16, "e": 16, "h": 0}
 W1_PIECES = [(0, 128), (128, 320), (320, N)]
 
 STRETCHES = [(0, 256), (256, 512), (512, 768), (768, U)]
-LAST_SPLIT = 832
+LAST_SPLIT = 896
 LONG = 3
 STORES = [(0, 512), (512, 768), (768, U)]
 
@@ -139,8 +139,9 @@ def tile_picked_edgeatt_sigmoid_po_kernel(
 
         w1_mx = mx_tiles("w1")
 
-        for piece in w1_raw[:-1]:
-            deal(w1_mx, piece, 0, PACK)
+        deal(w1_mx, w1_raw[0], 0, PACK)
+        deal(w1_mx, w1_raw[1], 0, 2)
+        deal(w1_mx, w1_raw[1], 2, PACK, nc.gpsimd.tensor_copy)
         deal(w1_mx, w1_raw[-1], 0, 1)
         quantise(w1_mx, 0, 1)
         deal(w1_mx, w1_raw[-1], 1, PACK)

@@ -23,14 +23,13 @@ BANK = 512
 LIST_ROWS = 16
 QUADRANTS = 4
 
-SPARE = {"y": 16, "e": 16, "h": 0}
+SPARE = {"y": LIST_ROWS, "e": LIST_ROWS, "h": 0}
 
 W1_PIECES = [(0, 128), (128, 320), (320, N)]
 
-STRETCHES = [(0, 256), (256, 512), (512, 768), (768, U)]
-LAST_SPLIT = 896
-LONG = 3
-STORES = [(0, 512), (512, 768), (768, U)]
+STEP = 256
+WIDE = U - STEP
+LAST_SPLIT = 864
 
 
 def tile_picked_edgeatt_sigmoid_po_kernel(
@@ -101,13 +100,14 @@ def tile_picked_edgeatt_sigmoid_po_kernel(
         nc.vector.tensor_copy(x_bytes[:], scales_all[:].indirect(offs_sb[:]))
         nc.vector.tensor_copy(x_codes[:], words_all[:].indirect(offs_sb[:]))
 
-        by_banks = [(0, BANK, nc.scalar.copy), (BANK, S, nc.scalar.copy)]
-        shared = [(0, BANK, nc.scalar.copy), (BANK, 768, nc.vector.tensor_copy), (768, S, nc.scalar.copy)]
+        by_scalar = [(0, BANK, nc.scalar.copy), (BANK, S, nc.scalar.copy)]
         by_vector = [(0, BANK, nc.vector.tensor_copy), (BANK, S, nc.vector.tensor_copy)]
+        quarter = S - S // 4
+        by_both = [(0, BANK, nc.scalar.copy), (BANK, quarter, nc.vector.tensor_copy), (quarter, S, nc.scalar.copy)]
 
-        def product(weight, t, name, cuts, tag=None):
+        def product(weight, t, name, cuts, buffer=None):
             codes, scales = weight[1], weight[2]
-            rows = keep.tile([P, S + SPARE[name]], F32, name=tag or f"{name}{t}")
+            rows = keep.tile([P, S + SPARE[name]], F32, name=buffer or f"{name}{t}")
             if SPARE[name]:
                 nc.vector.memset(rows[:, S:], 0.0)
             for c0, c1, copy in cuts:
@@ -151,23 +151,23 @@ def tile_picked_edgeatt_sigmoid_po_kernel(
         w2_mx = mx_tiles("w2")
         deal(w2_mx, w2_raw, 0, PACK, nc.gpsimd.tensor_copy)
         for t in range(PACK - 1):
-            fetch_y(product(w1_mx, t, "y", by_vector if t else shared), t)
+            fetch_y(product(w1_mx, t, "y", by_vector if t else by_both), t)
         quantise(w2_mx, 0, PACK)
-        fetch_y(product(w1_mx, PACK - 1, "y", by_vector, tag="w2_raw0"), PACK - 1)
+        fetch_y(product(w1_mx, PACK - 1, "y", by_vector, buffer="w2_raw0"), PACK - 1)
         w3_mx = mx_tiles("w3")
         deal(w3_mx, w3_raw, 0, PACK, nc.gpsimd.tensor_copy)
         e = [product(w2_mx, t, "e", by_vector) for t in range(2)]
         quantise(w3_mx, 0, PACK)
-        e.extend(product(w2_mx, t, "e", by_banks) for t in range(2, PACK))
+        e.extend(product(w2_mx, t, "e", by_scalar) for t in range(2, PACK))
         for t in range(PACK):
             add_e(e[t], t)
 
-        wide = STRETCHES[LONG][0]
+        last = PACK - 1
         h = []
         for t in range(PACK):
-            h.append(product(w3_mx, t, "h", by_banks))
-            squash(t, t + 1, 0, wide if t < PACK - 1 else STRETCHES[0][1])
-        squash(PACK - 1, PACK, STRETCHES[0][1], wide)
+            h.append(product(w3_mx, t, "h", by_scalar))
+            squash(t, t + 1, 0, WIDE if t < last else STEP)
+        squash(last, PACK, STEP, WIDE)
 
         out_codes = keep.tile([P, U], U32, name="out_codes", align_bytes=64)
         out_scales = keep.tile([P, U], U8, name="out_scales", align_bytes=64)
@@ -175,9 +175,6 @@ def tile_picked_edgeatt_sigmoid_po_kernel(
         out_rows = out_0.rearrange("(p t) c -> p t c", t=PACK)
         out_words = out_1[0].rearrange("p c r -> p (c r)").bitcast(I32)
         msg = keep.tile([P, PACK, U], F32, name="msg")
-
-        def gates(c0, c1):
-            squash(0, PACK, c0, c1)
 
         def messages(tiles, c0, c1):
             for t in tiles:
@@ -204,26 +201,33 @@ def tile_picked_edgeatt_sigmoid_po_kernel(
         def store_words(queue, c0, c1):
             queue.dma_start(out_words[:, c0:c1], out_codes[:, c0:c1].bitcast(I32))
 
-        messages([0, 1], 0, wide)
-        store_rows(0, 2, 0, wide)
-        messages([2], 0, wide)
-        for c0, c1 in STRETCHES[:LONG]:
-            messages([PACK - 1], c0, c1)
-        store_rows(2, PACK, 0, wide)
-        gates(*STRETCHES[3])
-        for t in (0, 2):
-            messages([t, t + 1], wide, U)
-            store_rows(t, t + 2, wide, U)
-        for c0, c1 in STRETCHES[:LONG]:
-            round_edges(nc.scalar.copy, c0, c1)
-        round_edges(nc.scalar.copy, wide, LAST_SPLIT)
-        planes(*STORES[0])
-        store_words(nc.sync, *STORES[0])
+        messages([0, 1], 0, WIDE)
+        store_rows(0, 2, 0, WIDE)
+        messages([2], 0, WIDE)
+        for c0 in range(0, WIDE, STEP):
+            messages([last], c0, c0 + STEP)
+        store_rows(2, PACK, 0, WIDE)
+
+        squash(0, PACK, WIDE, U)
+        h_src = keep.tile([P, STEP], F32, name="h_src")
+        nc.scalar.activation(h_src[:], h[last][:].indirect(entries(src_sb, WIDE, STEP)), COPY)
+        messages([0, 1], WIDE, U)
+        store_rows(0, 2, WIDE, U)
+        messages([2], WIDE, U)
+        nc.vector.tensor_tensor(msg[:, last, WIDE:], h_src[:], gate[:, last, WIDE:], MULT)
+        store_rows(2, PACK, WIDE, U)
+
+        for c0 in range(0, WIDE, STEP):
+            round_edges(nc.scalar.copy, c0, c0 + STEP)
+        round_edges(nc.scalar.copy, WIDE, LAST_SPLIT)
+
+        planes(0, 2 * STEP)
+        store_words(nc.sync, 0, 2 * STEP)
         round_edges(nc.vector.tensor_copy, LAST_SPLIT, U)
-        planes(*STORES[1])
-        store_words(nc.sync, *STORES[1])
-        planes(STORES[2][0], U)
-        store_words(nc.scalar, STORES[2][0], U)
+        planes(2 * STEP, WIDE)
+        store_words(nc.sync, 2 * STEP, WIDE)
+        planes(WIDE, U)
+        store_words(nc.scalar, WIDE, U)
         for q in range(QUADRANTS):
             queue = nc.scalar if q == QUADRANTS - 1 else nc.sync
             queue.dma_start(

@@ -65,7 +65,7 @@ def tile_picked_edgeatt_sigmoid_po_kernel(
         nc.sync.dma_start(words_all[:].bitcast(I32), x_words[0].rearrange("p c r -> p (c r)").bitcast(I32))
         w1_raw.extend(load_weight(w1, "w1", c0, c1) for c0, c1 in W1_PIECES[1:])
         nc.sync.dma_start(dst_sb[:], dst)
-        w2_raw = load_weight(w2, "w2", 0, N)
+        w2_raw = [load_weight(w2, "w2", c0, c0 + N // 2) for c0 in (0, N // 2)]
         nc.sync.dma_start(src_sb[:], src)
         w3_raw = load_weight(w3, "w3", 0, N)
 
@@ -125,7 +125,6 @@ def tile_picked_edgeatt_sigmoid_po_kernel(
             return rows
 
         y_dst = [keep.tile([P, U], F32, name="y_dst", bufs=PACK - 1) for t in range(PACK)]
-        logit = keep.tile([P, PACK, U], F32, name="logit")
         gate = keep.tile([P, PACK, U], F32, name="gate")
 
         def fetch_y(y, t):
@@ -149,15 +148,17 @@ def tile_picked_edgeatt_sigmoid_po_kernel(
         quantise(w1_mx, 2, PACK)
 
         w2_mx = mx_tiles("w2")
-        deal(w2_mx, w2_raw, 0, PACK, nc.gpsimd.tensor_copy)
+        for half in w2_raw:
+            deal(w2_mx, half, 0, PACK, nc.gpsimd.tensor_copy)
         for t in range(PACK - 1):
             fetch_y(product(w1_mx, t, "y", by_vector if t else by_both), t)
         quantise(w2_mx, 0, PACK)
-        fetch_y(product(w1_mx, PACK - 1, "y", by_vector, buffer="w2_raw0"), PACK - 1)
+        fetch_y(product(w1_mx, PACK - 1, "y", by_vector, buffer="w2_raw256"), PACK - 1)
         w3_mx = mx_tiles("w3")
         deal(w3_mx, w3_raw, 0, PACK, nc.gpsimd.tensor_copy)
         e = [product(w2_mx, t, "e", by_vector) for t in range(2)]
         quantise(w3_mx, 0, PACK)
+        logit = keep.tile([P, PACK, U], F32, name="w3_raw0")
         e.extend(product(w2_mx, t, "e", by_scalar) for t in range(2, PACK))
         for t in range(PACK):
             add_e(e[t], t)
@@ -212,10 +213,9 @@ def tile_picked_edgeatt_sigmoid_po_kernel(
         h_src = keep.tile([P, STEP], F32, name="h_src")
         nc.scalar.activation(h_src[:], h[last][:].indirect(entries(src_sb, WIDE, STEP)), COPY)
         messages([0, 1], WIDE, U)
-        store_rows(0, 2, WIDE, U)
         messages([2], WIDE, U)
         nc.vector.tensor_tensor(msg[:, last, WIDE:], h_src[:], gate[:, last, WIDE:], MULT)
-        store_rows(2, PACK, WIDE, U)
+        store_rows(0, PACK, WIDE, U)
 
         for c0 in range(0, WIDE, STEP):
             round_edges(nc.scalar.copy, c0, c0 + STEP)

@@ -29,7 +29,7 @@ W1_PIECES = [(0, 128), (128, 320), (320, N)]
 
 STEP = 256
 WIDE = U - STEP
-LAST_SPLIT = 864
+LAST_SPLIT = 896
 
 
 def tile_picked_edgeatt_sigmoid_po_kernel(
@@ -175,21 +175,25 @@ def tile_picked_edgeatt_sigmoid_po_kernel(
         rounded = keep.tile([P, U * PACK], BF16, name="rounded", align_bytes=64)
         out_rows = out_0.rearrange("(p t) c -> p t c", t=PACK)
         out_words = out_1[0].rearrange("p c r -> p (c r)").bitcast(I32)
-        msg = keep.tile([P, PACK, U], F32, name="msg")
+        msg_wide = keep.tile([P, PACK, WIDE], F32, name="msg_wide")
+        msg_last = keep.tile([P, PACK, STEP], F32, name="msg_last")
+
+        def msg(t0, t1, c0, c1):
+            return msg_wide[:, t0:t1, c0:c1] if c0 < WIDE else msg_last[:, t0:t1, c0 - WIDE : c1 - WIDE]
 
         def messages(tiles, c0, c1):
             for t in tiles:
                 nc.vector.tensor_tensor(
-                    msg[:, t, c0:c1], h[t][:].indirect(entries(src_sb, c0, c1 - c0)), gate[:, t, c0:c1], MULT
+                    msg(t, t + 1, c0, c1)[:, 0, :], h[t][:].indirect(entries(src_sb, c0, c1 - c0)), gate[:, t, c0:c1], MULT
                 )
 
         def store_rows(t0, t1, c0, c1):
-            nc.sync.dma_start(out_rows[:, t0:t1, c0:c1], msg[:, t0:t1, c0:c1])
+            nc.sync.dma_start(out_rows[:, t0:t1, c0:c1], msg(t0, t1, c0, c1))
 
         def round_edges(copy, c0, c1):
             copy(
-                rounded[:, PACK * c0 : PACK * c1].rearrange("p (c i t) -> p c t i", i=4, t=PACK),
-                msg[:, :, c0:c1].rearrange("p t (c i) -> p c t i", i=4),
+                rounded[:, PACK * c0 : PACK * c1].rearrange("p (c i t) -> p c t i", i=2, t=PACK),
+                msg(0, PACK, c0, c1).rearrange("p t (c i) -> p c t i", i=2),
             )
 
         def planes(c0, c1):
@@ -214,7 +218,7 @@ def tile_picked_edgeatt_sigmoid_po_kernel(
         nc.scalar.activation(h_src[:], h[last][:].indirect(entries(src_sb, WIDE, STEP)), COPY)
         messages([0, 1], WIDE, U)
         messages([2], WIDE, U)
-        nc.vector.tensor_tensor(msg[:, last, WIDE:], h_src[:], gate[:, last, WIDE:], MULT)
+        nc.vector.tensor_tensor(msg_last[:, last, :], h_src[:], gate[:, last, WIDE:], MULT)
         store_rows(0, PACK, WIDE, U)
 
         for c0 in range(0, WIDE, STEP):

@@ -209,17 +209,19 @@ def tile_picked_edgeatt_sigmoid_po_kernel(
         messages([0, 1], 0, WIDE)
         store_rows(0, 2, 0, WIDE)
         messages([2], 0, WIDE)
+        store_rows(2, last, 0, WIDE)
         for c0 in range(0, WIDE, STEP):
             messages([last], c0, c0 + STEP)
-        store_rows(2, PACK, 0, WIDE)
+        store_rows(last, PACK, 0, WIDE)
 
         squash(0, PACK, WIDE, U)
         h_src = keep.tile([P, STEP], F32, name="h_src")
         nc.scalar.activation(h_src[:], h[last][:].indirect(entries(src_sb, WIDE, STEP)), COPY)
         messages([0, 1], WIDE, U)
+        store_rows(0, 2, WIDE, U)
         messages([2], WIDE, U)
         nc.vector.tensor_tensor(msg_last[:, last, :], h_src[:], gate[:, last, WIDE:], MULT)
-        store_rows(0, PACK, WIDE, U)
+        store_rows(2, PACK, WIDE, U)
 
         for c0 in range(0, WIDE, STEP):
             round_edges(nc.scalar.copy, c0, c0 + STEP)

@@ -231,9 +231,8 @@ def tile_picked_edgeatt_sigmoid_po_kernel(
         store_words(nc.sync, 0, 2 * STEP)
         round_edges(nc.vector.tensor_copy, LAST_SPLIT, U)
         planes(2 * STEP, WIDE)
-        store_words(nc.sync, 2 * STEP, WIDE)
         planes(WIDE, U)
-        store_words(nc.scalar, WIDE, U)
+        store_words(nc.scalar, 2 * STEP, U)
         for q in range(QUADRANTS):
             queue = nc.scalar if q == QUADRANTS - 1 else nc.sync
             queue.dma_start(

@@ -25,7 +25,8 @@ QUADRANTS = 4
 
 SPARE = {"y": LIST_ROWS, "e": LIST_ROWS, "h": 0}
 
-W1_PIECES = [(0, 128), (128, 320), (320, N)]
+QUARTER = S // 4
+DEAL_SPLIT = 80
 
 STEP = 256
 WIDE = U - STEP
@@ -56,17 +57,20 @@ def tile_picked_edgeatt_sigmoid_po_kernel(
             nc.sync.dma_start(raw[:], w.rearrange("(p j) c -> p j c", j=PACK)[:, :, c0:c1])
             return raw, c0, c1
 
+        w2_rows = w2.rearrange("(p j) c -> p j c", j=PACK)
+        w2_raw = keep.tile([P, PACK, N], F32, name="w2_raw")
+        nc.sync.dma_start(w2_raw[:, 0, :], w2_rows[:, 0, :])
         nc.sync.dma_start(offs_sb[:], offs)
-        w1_raw = [load_weight(w1, "w1", *W1_PIECES[0])]
         for q in range(QUADRANTS):
             nc.sync.dma_start(
                 scales_all[32 * q : 32 * q + 4, :].bitcast(I32), x_scales[0, 4 * q : 4 * q + 4, :].bitcast(I32)
             )
+        nc.sync.dma_start(w2_raw[:, 1:, :], w2_rows[:, 1:, :])
         nc.sync.dma_start(words_all[:].bitcast(I32), x_words[0].rearrange("p c r -> p (c r)").bitcast(I32))
-        w1_raw.extend(load_weight(w1, "w1", c0, c1) for c0, c1 in W1_PIECES[1:])
-        nc.sync.dma_start(dst_sb[:], dst)
-        w2_raw = [load_weight(w2, "w2", c0, c0 + N // 2) for c0 in (0, N // 2)]
+        w1_raw = [load_weight(w1, "w1", 0, N // 2)]
         nc.sync.dma_start(src_sb[:], src)
+        w1_raw.append(load_weight(w1, "w1", N // 2, N))
+        nc.sync.dma_start(dst_sb[:], dst)
         w3_raw = load_weight(w3, "w3", 0, N)
 
         table = keep.tile([P, 1], F32, name="table")
@@ -80,11 +84,13 @@ def tile_picked_edgeatt_sigmoid_po_kernel(
             scales = keep.tile([P, N], U8, name=f"{name}_scales", align_bytes=64)
             return dealt, codes, scales
 
-        def deal(weight, piece, t0, t1, copy=nc.scalar.copy):
+        def deal(weight, piece, t0, t1, copy, m0=None, m1=None):
             raw, c0, c1 = piece
+            m0 = c0 // PACK if m0 is None else m0
+            m1 = c1 // PACK if m1 is None else m1
             copy(
-                weight[0][:, t0:t1, c0 // PACK : c1 // PACK, :].rearrange("p t m j -> p m t j"),
-                raw[:].rearrange("p j (m t) -> p m t j", t=PACK)[:, :, t0:t1, :],
+                weight[0][:, t0:t1, m0:m1, :].rearrange("p t m j -> p m t j"),
+                raw[:].rearrange("p j (m t) -> p m t j", t=PACK)[:, m0 - c0 // PACK : m1 - c0 // PACK, t0:t1, :],
             )
 
         def quantise(weight, t0, t1):
@@ -98,70 +104,79 @@ def tile_picked_edgeatt_sigmoid_po_kernel(
         x_codes = keep.tile([P, S], U32, name="x_codes", align_bytes=64)
         x_bytes = keep.tile([P, S], U8, name="x_bytes", align_bytes=64)
         nc.vector.tensor_copy(x_bytes[:], scales_all[:].indirect(offs_sb[:]))
-        nc.vector.tensor_copy(x_codes[:], words_all[:].indirect(offs_sb[:]))
 
         by_scalar = [(0, BANK, nc.scalar.copy), (BANK, S, nc.scalar.copy)]
         by_vector = [(0, BANK, nc.vector.tensor_copy), (BANK, S, nc.vector.tensor_copy)]
-        quarter = S - S // 4
-        by_both = [(0, BANK, nc.scalar.copy), (BANK, quarter, nc.vector.tensor_copy), (quarter, S, nc.scalar.copy)]
+        by_both = [(0, BANK, nc.vector.tensor_copy), (BANK, S, nc.scalar.copy)]
 
-        def product(weight, t, name, cuts, buffer=None):
-            codes, scales = weight[1], weight[2]
-            rows = keep.tile([P, S + SPARE[name]], F32, name=buffer or f"{name}{t}")
+        def window(name, t):
+            rows = keep.tile([P, S + SPARE[name]], F32, name=f"{name}{t}")
             if SPARE[name]:
                 nc.vector.memset(rows[:, S:], 0.0)
-            for c0, c1, copy in cuts:
-                acc = psum.tile([P, BANK], F32, name="acc")
-                nc.tensor.matmul_mx(
-                    out=acc[:, : c1 - c0],
-                    lhsT=codes[:, t * P : (t + 1) * P].bitcast(FP8X4),
-                    lhsT_scale=scales[:, t * P : (t + 1) * P],
-                    rhs=x_codes[:, c0:c1].bitcast(FP8X4),
-                    rhs_scale=x_bytes[:, c0:c1],
-                    start=True,
-                    stop=True,
-                )
-                copy(rows[:, c0:c1], acc[:, : c1 - c0])
             return rows
 
-        y_dst = [keep.tile([P, U], F32, name="y_dst", bufs=PACK - 1) for t in range(PACK)]
+        def piece(weight, t, rows, c0, c1, copy):
+            acc = psum.tile([P, BANK], F32, name="acc")
+            nc.tensor.matmul_mx(
+                out=acc[:, : c1 - c0],
+                lhsT=weight[1][:, t * P : (t + 1) * P].bitcast(FP8X4),
+                lhsT_scale=weight[2][:, t * P : (t + 1) * P],
+                rhs=x_codes[:, c0:c1].bitcast(FP8X4),
+                rhs_scale=x_bytes[:, c0:c1],
+                start=True,
+                stop=True,
+            )
+            copy(rows[:, c0:c1], acc[:, : c1 - c0])
+
+        def product(weight, t, name, cuts):
+            rows = window(name, t)
+            for c0, c1, copy in cuts:
+                piece(weight, t, rows, c0, c1, copy)
+            return rows
+
+        e_src = [keep.tile([P, U], F32, name="e_src", bufs=PACK - 1) for t in range(PACK)]
         gate = keep.tile([P, PACK, U], F32, name="gate")
 
-        def fetch_y(y, t):
-            nc.scalar.activation(y_dst[t][:], y[:].indirect(dst_sb[:]), COPY)
+        def fetch_e(e, t):
+            nc.scalar.activation(e_src[t][:], e[:].indirect(src_sb[:]), COPY)
 
-        def add_e(e, t):
-            nc.vector.tensor_tensor(logit[:, t, :], e[:].indirect(src_sb[:]), y_dst[t][:], ADD)
+        def add_y(y, t):
+            nc.vector.tensor_tensor(logit[:, t, :], y[:].indirect(dst_sb[:]), e_src[t][:], ADD)
 
         def squash(t0, t1, c0, c1):
             nc.scalar.activation(gate[:, t0:t1, c0:c1], logit[:, t0:t1, c0:c1], SIGMOID)
 
-        w1_mx = mx_tiles("w1")
-
-        deal(w1_mx, w1_raw[0], 0, PACK)
-        deal(w1_mx, w1_raw[1], 0, 2)
-        deal(w1_mx, w1_raw[1], 2, PACK, nc.gpsimd.tensor_copy)
-        deal(w1_mx, w1_raw[-1], 0, 1)
-        quantise(w1_mx, 0, 1)
-        deal(w1_mx, w1_raw[-1], 1, PACK)
-        quantise(w1_mx, 1, 2)
-        quantise(w1_mx, 2, PACK)
-
         w2_mx = mx_tiles("w2")
-        for half in w2_raw:
-            deal(w2_mx, half, 0, PACK, nc.gpsimd.tensor_copy)
-        for t in range(PACK - 1):
-            fetch_y(product(w1_mx, t, "y", by_vector if t else by_both), t)
-        quantise(w2_mx, 0, PACK)
-        fetch_y(product(w1_mx, PACK - 1, "y", by_vector, buffer="w2_raw256"), PACK - 1)
+        for t0 in (0, 2):
+            deal(w2_mx, (w2_raw, 0, N), t0, t0 + 2, nc.vector.tensor_copy, 0, DEAL_SPLIT)
+            deal(w2_mx, (w2_raw, 0, N), t0, t0 + 2, nc.scalar.copy, DEAL_SPLIT, P)
+        quantise(w2_mx, 0, 2)
+        quantise(w2_mx, 2, PACK)
+
+        w1_mx = mx_tiles("w1")
+        for half in w1_raw:
+            deal(w1_mx, half, 0, PACK, nc.gpsimd.tensor_copy)
+
+        e = [window("e", t) for t in range(2)]
+        for c0 in range(0, S, QUARTER):
+            nc.vector.tensor_copy(x_codes[:, c0 : c0 + QUARTER], words_all[:].indirect(entries(offs_sb, c0, QUARTER)))
+            piece(w2_mx, 0, e[0], c0, c0 + QUARTER, nc.scalar.copy)
+            piece(w2_mx, 1, e[1], c0, c0 + QUARTER, nc.scalar.copy if c0 + QUARTER < S else nc.vector.tensor_copy)
+        fetch_e(e[0], 0)
+        fetch_e(e[1], 1)
+        for t in range(2, PACK):
+            e.append(product(w2_mx, t, "e", by_vector if t == 2 else by_both))
+        fetch_e(e[2], 2)
+        quantise(w1_mx, 0, PACK)
         w3_mx = mx_tiles("w3")
         deal(w3_mx, w3_raw, 0, PACK, nc.gpsimd.tensor_copy)
-        e = [product(w2_mx, t, "e", by_vector) for t in range(2)]
+        y = [product(w1_mx, t, "y", cuts) for t, cuts in enumerate([by_vector, by_vector, by_both, by_scalar])]
         quantise(w3_mx, 0, PACK)
         logit = keep.tile([P, PACK, U], F32, name="w3_raw0")
-        e.extend(product(w2_mx, t, "e", by_scalar) for t in range(2, PACK))
-        for t in range(PACK):
-            add_e(e[t], t)
+        add_y(y[0], 0)
+        fetch_e(e[3], 3)
+        for t in range(1, PACK):
+            add_y(y[t], t)
 
         last = PACK - 1
         h = []

@@ -26,8 +26,6 @@ QUADRANTS = 4
 SPARE = {"y": LIST_ROWS, "e": LIST_ROWS, "h": 0}
 
 QUARTER = S // 4
-DEAL_SPLIT = 80
-
 STEP = 256
 WIDE = U - STEP
 LAST_SPLIT = 896
@@ -84,13 +82,12 @@ def tile_picked_edgeatt_sigmoid_po_kernel(
             scales = keep.tile([P, N], U8, name=f"{name}_scales", align_bytes=64)
             return dealt, codes, scales
 
-        def deal(weight, piece, t0, t1, copy, m0=None, m1=None):
-            raw, c0, c1 = piece
-            m0 = c0 // PACK if m0 is None else m0
-            m1 = c1 // PACK if m1 is None else m1
+        def deal(weight, piece, copy, c0=None, c1=None):
+            raw, first, end = piece
+            c0, c1 = (first, end) if c0 is None else (c0, c1)
             copy(
-                weight[0][:, t0:t1, m0:m1, :].rearrange("p t m j -> p m t j"),
-                raw[:].rearrange("p j (m t) -> p m t j", t=PACK)[:, m0 - c0 // PACK : m1 - c0 // PACK, t0:t1, :],
+                weight[0][:, :, c0 // PACK : c1 // PACK, :].rearrange("p t m (u j) -> p m u t j", j=2),
+                raw[:, :, c0 - first : c1 - first].rearrange("p (u j) (m t) -> p m u t j", j=2, t=PACK),
             )
 
         def quantise(weight, t0, t1):
@@ -107,10 +104,10 @@ def tile_picked_edgeatt_sigmoid_po_kernel(
 
         by_scalar = [(0, BANK, nc.scalar.copy), (BANK, S, nc.scalar.copy)]
         by_vector = [(0, BANK, nc.vector.tensor_copy), (BANK, S, nc.vector.tensor_copy)]
-        by_both = [(0, BANK, nc.vector.tensor_copy), (BANK, S, nc.scalar.copy)]
+        by_both = [by_vector[0], by_scalar[1]]
 
-        def window(name, t):
-            rows = keep.tile([P, S + SPARE[name]], F32, name=f"{name}{t}")
+        def window(name, t, buffer=None):
+            rows = keep.tile([P, S + SPARE[name]], F32, name=buffer or f"{name}{t}")
             if SPARE[name]:
                 nc.vector.memset(rows[:, S:], 0.0)
             return rows
@@ -128,13 +125,13 @@ def tile_picked_edgeatt_sigmoid_po_kernel(
             )
             copy(rows[:, c0:c1], acc[:, : c1 - c0])
 
-        def product(weight, t, name, cuts):
-            rows = window(name, t)
+        def product(weight, t, name, cuts, buffer=None):
+            rows = window(name, t, buffer)
             for c0, c1, copy in cuts:
                 piece(weight, t, rows, c0, c1, copy)
             return rows
 
-        e_src = [keep.tile([P, U], F32, name="e_src", bufs=PACK - 1) for t in range(PACK)]
+        e_src = [keep.tile([P, U], F32, name=f"e_src{t}") for t in range(PACK - 1)]
         gate = keep.tile([P, PACK, U], F32, name="gate")
 
         def fetch_e(e, t):
@@ -147,15 +144,25 @@ def tile_picked_edgeatt_sigmoid_po_kernel(
             nc.scalar.activation(gate[:, t0:t1, c0:c1], logit[:, t0:t1, c0:c1], SIGMOID)
 
         w2_mx = mx_tiles("w2")
-        for t0 in (0, 2):
-            deal(w2_mx, (w2_raw, 0, N), t0, t0 + 2, nc.vector.tensor_copy, 0, DEAL_SPLIT)
-            deal(w2_mx, (w2_raw, 0, N), t0, t0 + 2, nc.scalar.copy, DEAL_SPLIT, P)
-        quantise(w2_mx, 0, 2)
-        quantise(w2_mx, 2, PACK)
+        deal(w2_mx, (w2_raw, 0, N), nc.scalar.copy, 0, N // 2)
+        deal(w2_mx, (w2_raw, 0, N), nc.gpsimd.tensor_copy, N // 2, N)
+        quantise(w2_mx, 0, PACK)
+
+        for t in range(2):
+            unread = psum.tile([P, BANK], F32, name="acc")
+            nc.tensor.matmul_mx(
+                out=unread[:],
+                lhsT=w2_mx[1][:, t * P : (t + 1) * P].bitcast(FP8X4),
+                lhsT_scale=w2_mx[2][:, t * P : (t + 1) * P],
+                rhs=w2_mx[1][:].bitcast(FP8X4),
+                rhs_scale=w2_mx[2][:],
+                start=True,
+                stop=True,
+            )
 
         w1_mx = mx_tiles("w1")
         for half in w1_raw:
-            deal(w1_mx, half, 0, PACK, nc.gpsimd.tensor_copy)
+            deal(w1_mx, half, nc.gpsimd.tensor_copy)
 
         e = [window("e", t) for t in range(2)]
         for c0 in range(0, S, QUARTER):
@@ -164,18 +171,18 @@ def tile_picked_edgeatt_sigmoid_po_kernel(
             piece(w2_mx, 1, e[1], c0, c0 + QUARTER, nc.scalar.copy if c0 + QUARTER < S else nc.vector.tensor_copy)
         fetch_e(e[0], 0)
         fetch_e(e[1], 1)
-        for t in range(2, PACK):
-            e.append(product(w2_mx, t, "e", by_vector if t == 2 else by_both))
+        e.append(product(w2_mx, 2, "e", by_vector))
         fetch_e(e[2], 2)
         quantise(w1_mx, 0, PACK)
+        e.append(product(w2_mx, 3, "e", by_vector, buffer="w1_raw256"))
         w3_mx = mx_tiles("w3")
-        deal(w3_mx, w3_raw, 0, PACK, nc.gpsimd.tensor_copy)
-        y = [product(w1_mx, t, "y", cuts) for t, cuts in enumerate([by_vector, by_vector, by_both, by_scalar])]
+        deal(w3_mx, w3_raw, nc.gpsimd.tensor_copy)
+        y = [product(w1_mx, t, "y", cuts) for t, cuts in enumerate([by_vector, by_both, by_scalar, by_scalar])]
         quantise(w3_mx, 0, PACK)
         logit = keep.tile([P, PACK, U], F32, name="w3_raw0")
-        add_y(y[0], 0)
+        e_src.append(keep.tile([P, U], F32, name="dealt", align_bytes=64))
         fetch_e(e[3], 3)
-        for t in range(1, PACK):
+        for t in range(PACK):
             add_y(y[t], t)
 
         last = PACK - 1
@@ -230,12 +237,9 @@ def tile_picked_edgeatt_sigmoid_po_kernel(
         store_rows(last, PACK, 0, WIDE)
 
         squash(0, PACK, WIDE, U)
-        h_src = keep.tile([P, STEP], F32, name="h_src")
-        nc.scalar.activation(h_src[:], h[last][:].indirect(entries(src_sb, WIDE, STEP)), COPY)
         messages([0, 1], WIDE, U)
         store_rows(0, 2, WIDE, U)
-        messages([2], WIDE, U)
-        nc.vector.tensor_tensor(msg_last[:, last, :], h_src[:], gate[:, last, WIDE:], MULT)
+        messages([2, last], WIDE, U)
         store_rows(2, PACK, WIDE, U)
 
         for c0 in range(0, WIDE, STEP):

@@ -68,8 +68,8 @@ def tile_picked_edgeatt_sigmoid_po_kernel(
         w1_raw = [load_weight(w1, "w1", 0, N // 2)]
         nc.sync.dma_start(src_sb[:], src)
         w1_raw.append(load_weight(w1, "w1", N // 2, N))
-        nc.sync.dma_start(dst_sb[:], dst)
         w3_raw = load_weight(w3, "w3", 0, N)
+        nc.sync.dma_start(dst_sb[:], dst)
 
         table = keep.tile([P, 1], F32, name="table")
         nc.gpsimd.memset(table[:], 0.0)
@@ -104,7 +104,7 @@ def tile_picked_edgeatt_sigmoid_po_kernel(
 
         by_scalar = [(0, BANK, nc.scalar.copy), (BANK, S, nc.scalar.copy)]
         by_vector = [(0, BANK, nc.vector.tensor_copy), (BANK, S, nc.vector.tensor_copy)]
-        by_both = [by_vector[0], by_scalar[1]]
+        by_both = [by_vector[0], (BANK, S - QUARTER, nc.vector.tensor_copy), (S - QUARTER, S, nc.scalar.copy)]
 
         def window(name, t, buffer=None):
             rows = keep.tile([P, S + SPARE[name]], F32, name=buffer or f"{name}{t}")
@@ -164,14 +164,15 @@ def tile_picked_edgeatt_sigmoid_po_kernel(
         for half in w1_raw:
             deal(w1_mx, half, nc.gpsimd.tensor_copy)
 
-        e = [window("e", t) for t in range(2)]
+        e = [window("e", t) for t in range(3)]
         for c0 in range(0, S, QUARTER):
             nc.vector.tensor_copy(x_codes[:, c0 : c0 + QUARTER], words_all[:].indirect(entries(offs_sb, c0, QUARTER)))
             piece(w2_mx, 0, e[0], c0, c0 + QUARTER, nc.scalar.copy)
-            piece(w2_mx, 1, e[1], c0, c0 + QUARTER, nc.scalar.copy if c0 + QUARTER < S else nc.vector.tensor_copy)
+            piece(w2_mx, 1, e[1], c0, c0 + QUARTER, nc.scalar.copy if c0 < BANK else nc.vector.tensor_copy)
+            if (c0 + QUARTER) % BANK == 0:
+                piece(w2_mx, 2, e[2], c0 + QUARTER - BANK, c0 + QUARTER, nc.vector.tensor_copy)
         fetch_e(e[0], 0)
         fetch_e(e[1], 1)
-        e.append(product(w2_mx, 2, "e", by_vector))
         fetch_e(e[2], 2)
         quantise(w1_mx, 0, PACK)
         e.append(product(w2_mx, 3, "e", by_vector, buffer="w1_raw256"))
@@ -237,9 +238,12 @@ def tile_picked_edgeatt_sigmoid_po_kernel(
         store_rows(last, PACK, 0, WIDE)
 
         squash(0, PACK, WIDE, U)
+        h_src = keep.tile([P, STEP], F32, name="h_src")
+        nc.scalar.activation(h_src[:], h[last][:].indirect(entries(src_sb, WIDE, STEP)), COPY)
         messages([0, 1], WIDE, U)
         store_rows(0, 2, WIDE, U)
-        messages([2, last], WIDE, U)
+        messages([2], WIDE, U)
+        nc.vector.tensor_tensor(msg_last[:, last, :], h_src[:], gate[:, last, WIDE:], MULT)
         store_rows(2, PACK, WIDE, U)
 
         for c0 in range(0, WIDE, STEP):

@@ -148,18 +148,6 @@ def tile_picked_edgeatt_sigmoid_po_kernel(
         deal(w2_mx, (w2_raw, 0, N), nc.gpsimd.tensor_copy, N // 2, N)
         quantise(w2_mx, 0, PACK)
 
-        for t in range(2):
-            unread = psum.tile([P, BANK], F32, name="acc")
-            nc.tensor.matmul_mx(
-                out=unread[:],
-                lhsT=w2_mx[1][:, t * P : (t + 1) * P].bitcast(FP8X4),
-                lhsT_scale=w2_mx[2][:, t * P : (t + 1) * P],
-                rhs=w2_mx[1][:].bitcast(FP8X4),
-                rhs_scale=w2_mx[2][:],
-                start=True,
-                stop=True,
-            )
-
         w1_mx = mx_tiles("w1")
         for half in w1_raw:
             deal(w1_mx, half, nc.gpsimd.tensor_copy)

from contextlib import ExitStack

import concourse.mybir as mybir

K, T, S, N, U = 512, 2048, 1024, 512, 1024
FLOPS = 3 * 2 * K * N * S

F32 = mybir.dt.float32
BF16 = mybir.dt.bfloat16
I32 = mybir.dt.int32
U32 = mybir.dt.uint32
U16 = mybir.dt.uint16
U8 = mybir.dt.uint8
FP8X4 = mybir.dt.float8_e4m3fn_x4
ADD = mybir.AluOpType.add
MULT = mybir.AluOpType.mult
SIGMOID = mybir.ActivationFunctionType.Sigmoid
COPY = mybir.ActivationFunctionType.Copy

P = 128
PACK = 4
BANK = 512
LIST_ROWS = 16
QUADRANTS = 4

SPARE = {"y": LIST_ROWS, "e": LIST_ROWS, "h": 0}

QUARTER = S // 4
STEP = 256
WIDE = U - STEP
LAST_SPLIT = 896


def tile_picked_edgeatt_sigmoid_po_kernel(
    tc, x_words, x_scales, w1, w2, w3, offs, src, dst, out_0, out_1, out_2
):
    nc = tc.nc
    with ExitStack() as ctx:
        keep = ctx.enter_context(tc.tile_pool(name="keep", bufs=1))
        psum = ctx.enter_context(tc.psum_pool(name="psum", bufs=8))

        def entries(lst, first, count):
            return lst[:, first // LIST_ROWS : (first + count) // LIST_ROWS]

        offs_sb = keep.tile([P, S // LIST_ROWS], U16, name="offs_sb")
        src_sb = keep.tile([P, U // LIST_ROWS], U16, name="src_sb")
        dst_sb = keep.tile([P, U // LIST_ROWS], U16, name="dst_sb")
        words_all = keep.tile([P, T], U32, name="words_all", align_bytes=64)
        scales_all = keep.tile([P, T], U8, name="scales_all", align_bytes=64)

        nc.vector.memset(scales_all[:].bitcast(I32), 0)

        def load_weight(w, name, c0, c1):
            raw = keep.tile([P, PACK, c1 - c0], F32, name=f"{name}_raw{c0}")
            nc.sync.dma_start(raw[:], w.rearrange("(p j) c -> p j c", j=PACK)[:, :, c0:c1])
            return raw, c0, c1

        w2_rows = w2.rearrange("(p j) c -> p j c", j=PACK)
        w2_raw = keep.tile([P, PACK, N], F32, name="w2_raw")
        nc.sync.dma_start(w2_raw[:, 0, :], w2_rows[:, 0, :])
        nc.sync.dma_start(offs_sb[:], offs)
        for q in range(QUADRANTS):
            nc.sync.dma_start(
                scales_all[32 * q : 32 * q + 4, :].bitcast(I32), x_scales[0, 4 * q : 4 * q + 4, :].bitcast(I32)
            )
        nc.sync.dma_start(w2_raw[:, 1:, :], w2_rows[:, 1:, :])
        nc.sync.dma_start(words_all[:].bitcast(I32), x_words[0].rearrange("p c r -> p (c r)").bitcast(I32))
        w1_raw = [load_weight(w1, "w1", 0, N // 2)]
        nc.sync.dma_start(src_sb[:], src)
        w1_raw.append(load_weight(w1, "w1", N // 2, N))
        w3_raw = load_weight(w3, "w3", 0, N)
        nc.sync.dma_start(dst_sb[:], dst)

        table = keep.tile([P, 1], F32, name="table")
        nc.gpsimd.memset(table[:], 0.0)
        table_out = keep.tile([P, 1], F32, name="table_out")
        nc.scalar.activation(table_out[:], table[:], SIGMOID)

        def mx_tiles(name):
            dealt = keep.tile([P, PACK, P, PACK], BF16, name="dealt", align_bytes=64)
            codes = keep.tile([P, N], U32, name=f"{name}_codes", align_bytes=64)
            scales = keep.tile([P, N], U8, name=f"{name}_scales", align_bytes=64)
            return dealt, codes, scales

        def deal(weight, piece, copy, c0=None, c1=None):
            raw, first, end = piece
            c0, c1 = (first, end) if c0 is None else (c0, c1)
            copy(
                weight[0][:, :, c0 // PACK : c1 // PACK, :].rearrange("p t m (u j) -> p m u t j", j=2),
                raw[:, :, c0 - first : c1 - first].rearrange("p (u j) (m t) -> p m u t j", j=2, t=PACK),
            )

        def quantise(weight, t0, t1):
            dealt, codes, scales = weight
            nc.vector.quantize_mx(
                out=codes[:, t0 * P : t1 * P].bitcast(FP8X4),
                scales=scales[:, t0 * P : t1 * P],
                in_=dealt[:, t0:t1, :, :].rearrange("p t m j -> p (t m j)"),
            )

        x_codes = keep.tile([P, S], U32, name="x_codes", align_bytes=64)
        x_bytes = keep.tile([P, S], U8, name="x_bytes", align_bytes=64)
        nc.vector.tensor_copy(x_bytes[:], scales_all[:].indirect(offs_sb[:]))

        by_scalar = [(0, BANK, nc.scalar.copy), (BANK, S, nc.scalar.copy)]
        by_vector = [(0, BANK, nc.vector.tensor_copy), (BANK, S, nc.vector.tensor_copy)]
        by_both = [by_vector[0], (BANK, S - QUARTER, nc.vector.tensor_copy), (S - QUARTER, S, nc.scalar.copy)]

        def window(name, t, buffer=None):
            rows = keep.tile([P, S + SPARE[name]], F32, name=buffer or f"{name}{t}")
            if SPARE[name]:
                nc.vector.memset(rows[:, S:], 0.0)
            return rows

        def piece(weight, t, rows, c0, c1, copy):
            acc = psum.tile([P, BANK], F32, name="acc")
            nc.tensor.matmul_mx(
                out=acc[:, : c1 - c0],
                lhsT=weight[1][:, t * P : (t + 1) * P].bitcast(FP8X4),
                lhsT_scale=weight[2][:, t * P : (t + 1) * P],
                rhs=x_codes[:, c0:c1].bitcast(FP8X4),
                rhs_scale=x_bytes[:, c0:c1],
                start=True,
                stop=True,
            )
            copy(rows[:, c0:c1], acc[:, : c1 - c0])

        def product(weight, t, name, cuts, buffer=None):
            rows = window(name, t, buffer)
            for c0, c1, copy in cuts:
                piece(weight, t, rows, c0, c1, copy)
            return rows

        e_src = [keep.tile([P, U], F32, name=f"e_src{t}") for t in range(PACK - 1)]
        gate = keep.tile([P, PACK, U], F32, name="gate")

        def fetch_e(e, t):
            nc.scalar.activation(e_src[t][:], e[:].indirect(src_sb[:]), COPY)

        def add_y(y, t):
            nc.vector.tensor_tensor(logit[:, t, :], y[:].indirect(dst_sb[:]), e_src[t][:], ADD)

        def squash(t0, t1, c0, c1):
            nc.scalar.activation(gate[:, t0:t1, c0:c1], logit[:, t0:t1, c0:c1], SIGMOID)

        w2_mx = mx_tiles("w2")
        deal(w2_mx, (w2_raw, 0, N), nc.scalar.copy, 0, N // 2)
        deal(w2_mx, (w2_raw, 0, N), nc.gpsimd.tensor_copy, N // 2, N)
        quantise(w2_mx, 0, PACK)

        w1_mx = mx_tiles("w1")
        for half in w1_raw:
            deal(w1_mx, half, nc.gpsimd.tensor_copy)

        e = [window("e", t) for t in range(3)]
        for c0 in range(0, S, QUARTER):
            nc.vector.tensor_copy(x_codes[:, c0 : c0 + QUARTER], words_all[:].indirect(entries(offs_sb, c0, QUARTER)))
            piece(w2_mx, 0, e[0], c0, c0 + QUARTER, nc.scalar.copy)
            piece(w2_mx, 1, e[1], c0, c0 + QUARTER, nc.scalar.copy if c0 < BANK else nc.vector.tensor_copy)
            if (c0 + QUARTER) % BANK == 0:
                piece(w2_mx, 2, e[2], c0 + QUARTER - BANK, c0 + QUARTER, nc.vector.tensor_copy)
        fetch_e(e[0], 0)
        fetch_e(e[1], 1)
        fetch_e(e[2], 2)
        quantise(w1_mx, 0, PACK)
        e.append(product(w2_mx, 3, "e", by_vector, buffer="w1_raw256"))
        w3_mx = mx_tiles("w3")
        deal(w3_mx, w3_raw, nc.gpsimd.tensor_copy)
        y = [product(w1_mx, t, "y", cuts) for t, cuts in enumerate([by_vector, by_both, by_scalar, by_scalar])]
        quantise(w3_mx, 0, PACK)
        logit = keep.tile([P, PACK, U], F32, name="w3_raw0")
        e_src.append(keep.tile([P, U], F32, name="dealt", align_bytes=64))
        fetch_e(e[3], 3)
        for t in range(PACK):
            add_y(y[t], t)

        last = PACK - 1
        h = []
        for t in range(PACK):
            h.append(product(w3_mx, t, "h", by_scalar))
            squash(t, t + 1, 0, WIDE if t < last else STEP)
        squash(last, PACK, STEP, WIDE)

        out_codes = keep.tile([P, U], U32, name="out_codes", align_bytes=64)
        out_scales = keep.tile([P, U], U8, name="out_scales", align_bytes=64)
        rounded = keep.tile([P, U * PACK], BF16, name="rounded", align_bytes=64)
        out_rows = out_0.rearrange("(p t) c -> p t c", t=PACK)
        out_words = out_1[0].rearrange("p c r -> p (c r)").bitcast(I32)
        msg_wide = keep.tile([P, PACK, WIDE], F32, name="msg_wide")
        msg_last = keep.tile([P, PACK, STEP], F32, name="msg_last")

        def msg(t0, t1, c0, c1):
            return msg_wide[:, t0:t1, c0:c1] if c0 < WIDE else msg_last[:, t0:t1, c0 - WIDE : c1 - WIDE]

        def messages(tiles, c0, c1):
            for t in tiles:
                nc.vector.tensor_tensor(
                    msg(t, t + 1, c0, c1)[:, 0, :], h[t][:].indirect(entries(src_sb, c0, c1 - c0)), gate[:, t, c0:c1], MULT
                )

        def store_rows(t0, t1, c0, c1):
            nc.sync.dma_start(out_rows[:, t0:t1, c0:c1], msg(t0, t1, c0, c1))

        def round_edges(copy, c0, c1):
            copy(
                rounded[:, PACK * c0 : PACK * c1].rearrange("p (c i t) -> p c t i", i=2, t=PACK),
                msg(0, PACK, c0, c1).rearrange("p t (c i) -> p c t i", i=2),
            )

        def planes(c0, c1):
            nc.vector.quantize_mx(
                out=out_codes[:, c0:c1].bitcast(FP8X4),
                scales=out_scales[:, c0:c1],
                in_=rounded[:, PACK * c0 : PACK * c1],
            )

        def store_words(queue, c0, c1):
            queue.dma_start(out_words[:, c0:c1], out_codes[:, c0:c1].bitcast(I32))

        messages([0, 1], 0, WIDE)
        store_rows(0, 2, 0, WIDE)
        messages([2], 0, WIDE)
        store_rows(2, last, 0, WIDE)
        for c0 in range(0, WIDE, STEP):
            messages([last], c0, c0 + STEP)
        store_rows(last, PACK, 0, WIDE)

        squash(0, PACK, WIDE, U)
        h_src = keep.tile([P, STEP], F32, name="h_src")
        nc.scalar.activation(h_src[:], h[last][:].indirect(entries(src_sb, WIDE, STEP)), COPY)
        messages([0, 1], WIDE, U)
        store_rows(0, 2, WIDE, U)
        messages([2], WIDE, U)
        nc.vector.tensor_tensor(msg_last[:, last, :], h_src[:], gate[:, last, WIDE:], MULT)
        store_rows(2, PACK, WIDE, U)

        for c0 in range(0, WIDE, STEP):
            round_edges(nc.scalar.copy, c0, c0 + STEP)
        round_edges(nc.scalar.copy, WIDE, LAST_SPLIT)

        planes(0, 2 * STEP)
        store_words(nc.sync, 0, 2 * STEP)
        round_edges(nc.vector.tensor_copy, LAST_SPLIT, U)
        planes(2 * STEP, WIDE)
        planes(WIDE, U)
        store_words(nc.scalar, 2 * STEP, U)
        for q in range(QUADRANTS):
            queue = nc.scalar if q == QUADRANTS - 1 else nc.sync
            queue.dma_start(
                out_2[0, 4 * q : 4 * q + 4, :].bitcast(I32), out_scales[32 * q : 32 * q + 4, :].bitcast(I32)
            )
